import numpy as np
import ml_dtypes


def mxq(x, axis, fmt="e4m3"):
    dtype, down = {"e4m3": (ml_dtypes.float8_e4m3fn, 7), "e5m2": (ml_dtypes.float8_e5m2, 14)}[fmt]
    v = np.moveaxis(np.asarray(x, np.float32).astype(ml_dtypes.bfloat16).astype(np.float64), axis, -1)
    blocks = v.reshape(v.shape[:-1] + (-1, 32))
    amax = np.abs(blocks).max(-1, keepdims=True)
    byte = np.maximum(np.where(amax > 0, np.frexp(amax)[1] - 1 + 127, 0) - down, 1)
    scale = np.exp2(byte - 127.0)
    codes = (blocks / scale).astype(np.float32).astype(dtype).astype(np.float64)
    return np.moveaxis((codes * scale).reshape(v.shape), -1, axis)


WIDE = False


def mx_kscale(k):
    if not WIDE:
        return np.ones(k)
    levels = np.array([10, -10, 5, -5, 0])
    if k % 512:
        return np.exp2(np.random.permutation(np.resize(levels, k // 32))).repeat(32)
    a = np.empty((k // 512, 16))
    for p in range(k // 512):
        a[p, :8] = np.random.permutation(np.resize(levels, 8))
        for g in range(8):
            far = levels[np.abs(levels - a[p, g]) >= 10]
            a[p, g + 8] = far[np.random.randint(len(far))]
    return np.exp2(a.ravel()).repeat(32)


def f64(x):
    return np.asarray(x).astype(np.float64)


def striped(idx):
    return np.tile(idx.reshape(-1, 16).T, (8, 1)).astype(np.uint16)


def unstriped(offs):
    return offs[:16].T.reshape(-1).astype(np.int64)


E2M1 = np.array([0.0, 0.5, 1.0, 1.5, 2.0, 3.0, 4.0, 6.0, -0.0, -0.5, -1.0, -1.5, -2.0, -3.0, -4.0, -6.0])


def pack_weight(w, fmt):
    k, n = w.shape
    w = f64(np.asarray(w, np.float32).astype(ml_dtypes.bfloat16)).reshape(k // 32, 32, n)
    amax = np.abs(w).max(1)
    if fmt == "e4m3":
        byte = np.frexp(amax)[1] - 1 + 127 - 7
    else:
        mant, ex = np.frexp(amax / 6.0)
        byte = np.where(mant > 0.5, ex, ex - 1) + 127
    byte = np.clip(np.where(amax > 0, byte, 1), 1, 254)
    scaled = (w * np.exp2(127.0 - byte)[:, None, :]).reshape(k, n).astype(np.float32)
    by_word = np.ascontiguousarray(scaled.reshape(k // 512, 128, 4, n).transpose(0, 1, 3, 2))
    if fmt == "e4m3":
        words = by_word.astype(ml_dtypes.float8_e4m3fn).view(np.uint8)
    else:
        c = by_word.astype(ml_dtypes.float4_e2m1fn).view(np.uint8) & 0xF
        words = (c[..., 0::2] | (c[..., 1::2] << 4)).reshape(k // 512, 128, 2 * n)
    return np.ascontiguousarray(words), np.ascontiguousarray(byte.astype(np.uint8).reshape(k // 512, 16, n))


def unpack_weight(words, scales, fmt):
    g, _, n = scales.shape
    words = np.ascontiguousarray(words).reshape(g, 128, n, -1)
    if fmt == "e4m3":
        vals = words.view(ml_dtypes.float8_e4m3fn).astype(np.float64)
    else:
        nib = np.empty((g, 128, n, 4), np.uint8)
        nib[..., 0::2] = words & 0xF
        nib[..., 1::2] = words >> 4
        vals = E2M1[nib]
    vals = vals * np.repeat(np.exp2(scales.astype(np.float64) - 127.0), 8, axis=1)[..., None]
    return vals.transpose(0, 1, 3, 2).reshape(g * 512, n)


def d_relu(v):
    return (v > 0).astype(np.float64)


K, T, E, C, H, N = 128, 640, 2, 256, 1024, 1536


def by_expert(wq, xq):
    return np.concatenate([wq[e].T @ xq[:, e * C:(e + 1) * C] for e in range(E)], axis=1)


def setup_inputs():
    n = np.random.standard_normal
    s = mx_kscale(N)[:, None]
    u = mx_kscale(H)
    w2 = [pack_weight(m, "e2m1") for m in n((E, N, H)) / np.sqrt(N) / s[None] * u[None, None, :]]
    w1 = [pack_weight(m, "e2m1") for m in n((E, H, K)) / np.sqrt(H) / u[None, :, None]]
    return {
        "dyT": (n((N, T)) * s).astype(np.float32),
        "a": n((H, E * C)).astype(np.float32),
        "w2_words": np.stack([m[0] for m in w2]),
        "w2_scales": np.stack([m[1] for m in w2]),
        "w1_words": np.stack([m[0] for m in w1]),
        "w1_scales": np.stack([m[1] for m in w1]),
        "gate": np.tile(np.random.uniform(0.2, 1.0, E * C), (N, 1)).astype(np.float32),
        "offs": striped(np.random.permutation(T)[:E * C]),
    }


def reference(dyT, a, w2_words, w2_scales, w1_words, w1_scales, gate, offs):
    idx = unstriped(offs)
    w2 = np.stack([unpack_weight(w2_words[e], w2_scales[e], "e2m1") for e in range(E)])
    w1 = np.stack([unpack_weight(w1_words[e], w1_scales[e], "e2m1") for e in range(E)])
    gq = mxq(f64(gate) * f64(dyT)[:, idx], 0, "e4m3")
    dh = by_expert(w2, gq)
    da = dh * d_relu(f64(a))
    dx = by_expert(w1, mxq(da, 0, "e4m3"))
    out = np.zeros((K, T))
    out[:, idx] = dx
    return out

@@ -1,0 +1,238 @@
+from contextlib import ExitStack
+
+import concourse.mybir as mybir
+from concourse.masks import make_identity
+
+K, T, E, C, H, N = 128, 640, 2, 256, 1024, 1536
+S = E * C
+FLOPS = 2 * S * (N * H + H * K)
+BYTES = 4 * (N * T + H * S + S + K * T) + E * (N * H + H * K) * 17 // 32 + 2 * S
+
+F32 = mybir.dt.float32
+BF16 = mybir.dt.bfloat16
+U32 = mybir.dt.uint32
+I32 = mybir.dt.int32
+U16 = mybir.dt.uint16
+U8 = mybir.dt.uint8
+E4M3 = mybir.dt.float8_e4m3fn_x4
+E2M1 = mybir.dt.float4_e2m1fn_x4
+MULT = mybir.AluOpType.mult
+IS_GT = mybir.AluOpType.is_gt
+
+P = 128
+PASSES = N // 512
+HALVES = H // 512
+GROUPS = S // P
+
+
+def tile_moe_bdx_mlp_relu_kernel(
+    tc, dyT, a, w2_words, w2_scales, w1_words, w1_scales, gate, offs, out
+):
+    nc = tc.nc
+    with ExitStack() as ctx:
+        held = ctx.enter_context(tc.tile_pool(name="held", bufs=1))
+        work = ctx.enter_context(tc.tile_pool(name="work", bufs=3))
+        dh_pool = ctx.enter_context(tc.psum_pool(name="dh_pool", bufs=5))
+        xt_pool = ctx.enter_context(tc.psum_pool(name="xt_pool", bufs=2))
+        o_pool = ctx.enter_context(tc.psum_pool(name="o_pool", bufs=1))
+
+        offsets = held.tile([P, S // 16], U16, name="offsets")
+        nc.sync.dma_start(offsets[:], offs)
+
+        gate_sb = [held.tile([P, C], F32, name=f"gate_sb{i}") for i in range(3)]
+        w2_planes = held.tile([P, E * PASSES, H], U8, name="w2_planes", align_bytes=64)
+        w1_planes = held.tile([P, E * HALVES, K], U8, name="w1_planes", align_bytes=64)
+        window = held.tile([P, T], F32, name="window")
+        identity = held.tile([P, P], F32, name="identity")
+        nc.gpsimd.memset(w2_planes[:].rearrange("p n c -> p (n c)").bitcast(I32), 0)
+        nc.gpsimd.memset(w1_planes[:].rearrange("p n c -> p (n c)").bitcast(I32), 0)
+        make_identity(nc, identity[:])
+        nc.gpsimd.memset(window[:], 0.0)
+
+        dy_view = dyT.rearrange("(s p d) t -> s d p t", p=P, d=4)
+        dy = [[held.tile([P, T], F32, name=f"dy{s}_{d}") for d in range(4)] for s in range(PASSES)]
+        w2_sb = [held.tile([P, PASSES, 2 * H], U8, name=f"w2_sb{e}", align_bytes=64) for e in range(E)]
+        w1_sb = held.tile([P, E * HALVES, 2 * K], U8, name="w1_sb", align_bytes=64)
+        a_sb = [held.tile([P, HALVES, 4, C], F32, name=f"a_sb{e}") for e in range(E)]
+        a_view = a.rearrange("(h p d) c -> h p d c", p=P, d=4)
+
+        def load_dy(s):
+            for d in range(4):
+                nc.sync.dma_start(dy[s][d][:], dy_view[s, d])
+
+        def load_w2(e):
+            nc.sync.dma_start(w2_sb[e][:].bitcast(I32), w2_words[e].rearrange("s p c -> p s c").bitcast(I32))
+
+        def load_a(e):
+            for h in range(HALVES):
+                nc.sync.dma_start(a_sb[e][:, h, :, :], a_view[h, :, :, e * C : (e + 1) * C])
+
+        def load_scales(planes, scales):
+            by_pass = scales.rearrange("e s f c -> (e s) f c")
+            for quad in range(4):
+                nc.sync.dma_start(
+                    planes[32 * quad : 32 * quad + 4, :, :].bitcast(I32),
+                    by_pass[:, 4 * quad : 4 * quad + 4, :].rearrange("n r c -> r n c").bitcast(I32),
+                )
+
+        nc.sync.dma_start(gate_sb[0][:], gate[0:P, 0:C])
+        load_dy(0)
+        load_dy(1)
+        nc.sync.dma_start(gate_sb[1][:], gate[0:P, C:S])
+        load_dy(2)
+        nc.sync.dma_start(gate_sb[2][:], gate[P : 2 * P, C:S])
+        load_w2(0)
+        load_scales(w2_planes, w2_scales)
+        load_scales(w1_planes, w1_scales)
+        load_w2(1)
+        load_a(0)
+        load_a(1)
+        nc.sync.dma_start(w1_sb[:].bitcast(I32), w1_words.rearrange("e s p c -> p (e s) c").bitcast(I32))
+
+        g_codes, g_scales, g_wide = {}, {}, {}
+
+        def gather(s, lo, n):
+            gate_of = gate_sb[0 if lo == 0 else 1 if s == 0 else 2]
+            g = work.tile([P, 4, n], F32, name="g")
+            for d in range(4):
+                nc.vector.tensor_tensor(
+                    g[:, d, :],
+                    dy[s][d][:].indirect(offsets[:, lo // 16 : (lo + n) // 16]),
+                    gate_of[:],
+                    MULT,
+                )
+            wide = work.tile([P, n, 4], BF16, name="wide", align_bytes=64)
+            nc.scalar.copy(
+                wide[:].rearrange("p (c i) d -> p c d i", i=4), g[:].rearrange("p d (c i) -> p c d i", i=4)
+            )
+            g_wide[s, lo] = wide
+
+        def quantize_g(s, lo, n):
+            codes = held.tile([P, n], U32, name=f"g_codes{s}_{lo}", align_bytes=64)
+            scales = held.tile([P, n], U8, name=f"g_scales{s}_{lo}", align_bytes=64)
+            nc.vector.quantize_mx(
+                out=codes[:].bitcast(E4M3), scales=scales[:], in_=g_wide[s, lo][:].rearrange("p c d -> p (c d)")
+            )
+            for q in range(lo // P, (lo + n) // P):
+                cols = slice(q * P - lo, q * P - lo + P)
+                g_codes[s, q] = codes[:, cols]
+                g_scales[s, q] = scales[:, cols]
+
+        dh, xts, live, das, codes2 = {}, {}, {}, {}, {}
+
+        def multiply_w2(q, passes):
+            e = q * P // C
+            for h in range(HALVES):
+                if 0 in passes:
+                    dh[q, h] = dh_pool.tile([P, 512], F32, name="dh")
+                for s in passes:
+                    nc.tensor.matmul_mx(
+                        out=dh[q, h][:],
+                        lhsT=g_codes[s, q].bitcast(E4M3),
+                        lhsT_scale=g_scales[s, q],
+                        rhs=w2_sb[e][:, s, 1024 * h : 1024 * (h + 1)].bitcast(E2M1),
+                        rhs_scale=w2_planes[:, e * PASSES + s, 512 * h : 512 * (h + 1)],
+                        start=(s == 0),
+                        stop=(s == PASSES - 1),
+                    )
+
+        def turn(q):
+            xts[q] = xt_pool.tile([P, HALVES, P, 2], F32, name="xt")
+            for h in range(HALVES):
+                dhb = work.tile([P, 2, 256], BF16, name="dhb")
+                nc.scalar.copy(
+                    dhb[:].rearrange("c u (p b) -> c u p b", b=2),
+                    dh[q, h][:].rearrange("c (p u b) -> c u p b", u=2, b=2),
+                )
+                for u in range(2):
+                    nc.tensor.transpose(xts[q][:, h, :, u], dhb[:, u, :].bitcast(F32), identity[:])
+
+        def make_mask(e):
+            live[e] = held.tile([P, HALVES, C, 4], BF16, name=f"mask{e}", tag=f"dy2_{3 - e}")
+            for h in range(HALVES):
+                nc.vector.tensor_scalar(
+                    live[e][:, h, :, :], a_sb[e][:, h, :, :].rearrange("p d c -> p c d"), 0.0, None, IS_GT
+                )
+
+        def mask(q):
+            e, lo = q * P // C, q * P % C
+            das[q] = work.tile([P, HALVES, P, 4], BF16, name="da", align_bytes=64)
+            nc.vector.tensor_tensor(
+                das[q][:].rearrange("p h c d -> p h (c d)"),
+                xts[q][:].rearrange("p h c u -> p h (c u)").bitcast(BF16),
+                live[e][:, :, lo : lo + P, :].rearrange("p h c d -> p h (c d)"),
+                MULT,
+            )
+
+        def quantize_da(q):
+            codes = work.tile([P, HALVES * P], U32, name="da_codes", align_bytes=64)
+            scales = work.tile([P, HALVES * P], U8, name="da_scales", align_bytes=64)
+            nc.vector.quantize_mx(
+                out=codes[:].bitcast(E4M3), scales=scales[:], in_=das[q][:].rearrange("p h c d -> p (h c d)")
+            )
+            codes2[q] = codes, scales
+
+        def multiply_w1(q, dx_sb):
+            e = q * P // C
+            codes, scales = codes2[q]
+            dx = o_pool.tile([P, P], F32, name="dx")
+            for h in range(HALVES):
+                cols = slice(h * P, (h + 1) * P)
+                nc.tensor.matmul_mx(
+                    out=dx[:],
+                    lhsT=w1_sb[:, e * HALVES + h, :].bitcast(E2M1),
+                    lhsT_scale=w1_planes[:, e * HALVES + h, :],
+                    rhs=codes[:, cols].bitcast(E4M3),
+                    rhs_scale=scales[:, cols],
+                    start=(h == 0),
+                    stop=(h == HALVES - 1),
+                )
+            nc.scalar.copy(dx_sb, dx[:])
+
+        def scatter(lo, n, dx_sb):
+            nc.vector.tensor_copy(window[:].indirect(offsets[:, lo // 16 : (lo + n) // 16]), dx_sb)
+
+        every = range(PASSES)
+        gather(0, 0, C)
+        gather(1, 0, C)
+        quantize_g(0, 0, C)
+        gather(2, 0, C)
+        quantize_g(1, 0, C)
+        gather(0, C, C)
+        quantize_g(2, 0, C)
+        multiply_w2(0, every)
+        multiply_w2(1, every)
+        gather(1, C, C)
+        turn(0)
+        gather(2, C, C)
+        turn(1)
+        quantize_g(0, C, C)
+        quantize_g(1, C, C)
+        multiply_w2(2, (0, 1))
+        multiply_w2(3, (0, 1))
+        make_mask(0)
+        mask(0)
+        quantize_g(2, C, C)
+        multiply_w2(2, (2,))
+        multiply_w2(3, (2,))
+        mask(1)
+        dx01 = held.tile([P, C], F32, name="dx01")
+        quantize_da(0)
+        multiply_w1(0, dx01[:, 0:P])
+        quantize_da(1)
+        multiply_w1(1, dx01[:, P:C])
+        turn(2)
+        make_mask(1)
+        turn(3)
+        scatter(0, C, dx01[:])
+        mask(2)
+        mask(3)
+        quantize_da(2)
+        dx2 = held.tile([P, P], F32, name="dx2")
+        multiply_w1(2, dx2[:])
+        quantize_da(3)
+        dx3 = held.tile([P, P], F32, name="dx3")
+        multiply_w1(3, dx3[:])
+        scatter(C, P, dx2[:])
+        scatter(C + P, P, dx3[:])
+        nc.sync.dma_start(out, window[:])

@@ -32,14 +32,14 @@ def tile_moe_bdx_mlp_relu_kernel(
     with ExitStack() as ctx:
         held = ctx.enter_context(tc.tile_pool(name="held", bufs=1))
         work = ctx.enter_context(tc.tile_pool(name="work", bufs=3))
-        dh_pool = ctx.enter_context(tc.psum_pool(name="dh_pool", bufs=5))
+        dh_pool = ctx.enter_context(tc.psum_pool(name="dh_pool", bufs=4))
         xt_pool = ctx.enter_context(tc.psum_pool(name="xt_pool", bufs=2))
-        o_pool = ctx.enter_context(tc.psum_pool(name="o_pool", bufs=1))
+        o_pool = ctx.enter_context(tc.psum_pool(name="o_pool", bufs=2))
 
         offsets = held.tile([P, S // 16], U16, name="offsets")
         nc.sync.dma_start(offsets[:], offs)
 
-        gate_sb = [held.tile([P, C], F32, name=f"gate_sb{i}") for i in range(3)]
+        gate_sb = [held.tile([P, C], F32, name=f"gate_sb{e}", align_bytes=64) for e in range(E)]
         w2_planes = held.tile([P, E * PASSES, H], U8, name="w2_planes", align_bytes=64)
         w1_planes = held.tile([P, E * HALVES, K], U8, name="w1_planes", align_bytes=64)
         window = held.tile([P, T], F32, name="window")
@@ -53,12 +53,15 @@ def tile_moe_bdx_mlp_relu_kernel(
         dy = [[held.tile([P, T], F32, name=f"dy{s}_{d}") for d in range(4)] for s in range(PASSES)]
         w2_sb = [held.tile([P, PASSES, 2 * H], U8, name=f"w2_sb{e}", align_bytes=64) for e in range(E)]
         w1_sb = held.tile([P, E * HALVES, 2 * K], U8, name="w1_sb", align_bytes=64)
-        a_sb = [held.tile([P, HALVES, 4, C], F32, name=f"a_sb{e}") for e in range(E)]
+        a_sb = [held.tile([P, HALVES, 4, C], F32, name=f"a_sb{e}", align_bytes=64) for e in range(E)]
         a_view = a.rearrange("(h p d) c -> h p d c", p=P, d=4)
 
         def load_dy(s):
             for d in range(4):
                 nc.sync.dma_start(dy[s][d][:], dy_view[s, d])
+
+        def load_gate(e):
+            nc.sync.dma_start(gate_sb[e][:], gate[0:P, e * C : (e + 1) * C])
 
         def load_w2(e):
             nc.sync.dma_start(w2_sb[e][:].bitcast(I32), w2_words[e].rearrange("s p c -> p s c").bitcast(I32))
@@ -75,46 +78,45 @@ def tile_moe_bdx_mlp_relu_kernel(
                     by_pass[:, 4 * quad : 4 * quad + 4, :].rearrange("n r c -> r n c").bitcast(I32),
                 )
 
-        nc.sync.dma_start(gate_sb[0][:], gate[0:P, 0:C])
+        load_gate(0)
         load_dy(0)
         load_dy(1)
-        nc.sync.dma_start(gate_sb[1][:], gate[0:P, C:S])
         load_dy(2)
-        nc.sync.dma_start(gate_sb[2][:], gate[P : 2 * P, C:S])
+        load_gate(1)
         load_w2(0)
         load_scales(w2_planes, w2_scales)
         load_scales(w1_planes, w1_scales)
-        load_w2(1)
         load_a(0)
-        load_a(1)
+        load_w2(1)
         nc.sync.dma_start(w1_sb[:].bitcast(I32), w1_words.rearrange("e s p c -> p (e s) c").bitcast(I32))
+        load_a(1)
 
-        g_codes, g_scales, g_wide = {}, {}, {}
+        g, g_wide, g_codes, g_scales = {}, {}, {}, {}
 
-        def gather(s, lo, n):
-            gate_of = gate_sb[0 if lo == 0 else 1 if s == 0 else 2]
-            g = work.tile([P, 4, n], F32, name="g")
+        def gather(s, e, tag=None):
+            g[s, e] = held.tile([P, 4 * C], F32, name=f"g{s}_{e}", tag=tag or f"g{s}_{e}", align_bytes=64)[:]
             for d in range(4):
                 nc.vector.tensor_tensor(
-                    g[:, d, :],
-                    dy[s][d][:].indirect(offsets[:, lo // 16 : (lo + n) // 16]),
-                    gate_of[:],
+                    g[s, e][:, d * C : (d + 1) * C],
+                    dy[s][d][:].indirect(offsets[:, e * C // 16 : (e + 1) * C // 16]),
+                    gate_sb[e][:],
                     MULT,
                 )
-            wide = work.tile([P, n, 4], BF16, name="wide", align_bytes=64)
-            nc.scalar.copy(
-                wide[:].rearrange("p (c i) d -> p c d i", i=4), g[:].rearrange("p d (c i) -> p c d i", i=4)
-            )
-            g_wide[s, lo] = wide
 
-        def quantize_g(s, lo, n):
-            codes = held.tile([P, n], U32, name=f"g_codes{s}_{lo}", align_bytes=64)
-            scales = held.tile([P, n], U8, name=f"g_scales{s}_{lo}", align_bytes=64)
-            nc.vector.quantize_mx(
-                out=codes[:].bitcast(E4M3), scales=scales[:], in_=g_wide[s, lo][:].rearrange("p c d -> p (c d)")
+        def interleave(s, e, wide=None):
+            if wide is None:
+                wide = held.tile([P, 4 * C], BF16, name=f"wide{s}_{e}", align_bytes=64)[:]
+            nc.scalar.copy(
+                wide.rearrange("p (c i d) -> p c d i", i=4, d=4), g[s, e].rearrange("p (d c i) -> p c d i", i=4, d=4)
             )
-            for q in range(lo // P, (lo + n) // P):
-                cols = slice(q * P - lo, q * P - lo + P)
+            g_wide[s, e] = wide
+
+        def quantize_g(s, e, tag=None):
+            codes = held.tile([P, C], U32, name=f"g_codes{s}_{e}", tag=tag or f"g_codes{s}_{e}", align_bytes=64)
+            scales = held.tile([P, C], U8, name=f"g_scales{s}_{e}", align_bytes=64)
+            nc.vector.quantize_mx(out=codes[:].bitcast(E4M3), scales=scales[:], in_=g_wide[s, e])
+            for q in range(2 * e, 2 * e + 2):
+                cols = slice(q * P - e * C, q * P - e * C + P)
                 g_codes[s, q] = codes[:, cols]
                 g_scales[s, q] = scales[:, cols]
 
@@ -136,29 +138,29 @@ def tile_moe_bdx_mlp_relu_kernel(
                         stop=(s == PASSES - 1),
                     )
 
-        def turn(q):
+        def turn(q, staging=None):
             xts[q] = xt_pool.tile([P, HALVES, P, 2], F32, name="xt")
             for h in range(HALVES):
-                dhb = work.tile([P, 2, 256], BF16, name="dhb")
+                if staging is None:
+                    dhb = work.tile([P, 512], BF16, name="dhb")[:]
+                else:
+                    dhb = staging[h]
                 nc.scalar.copy(
-                    dhb[:].rearrange("c u (p b) -> c u p b", b=2),
+                    dhb.rearrange("c (u p b) -> c u p b", u=2, b=2),
                     dh[q, h][:].rearrange("c (p u b) -> c u p b", u=2, b=2),
                 )
                 for u in range(2):
-                    nc.tensor.transpose(xts[q][:, h, :, u], dhb[:, u, :].bitcast(F32), identity[:])
+                    nc.tensor.transpose(xts[q][:, h, :, u], dhb[:, 256 * u : 256 * (u + 1)].bitcast(F32), identity[:])
 
-        def make_mask(e):
-            live[e] = held.tile([P, HALVES, C, 4], BF16, name=f"mask{e}", tag=f"dy2_{3 - e}")
-            for h in range(HALVES):
-                nc.vector.tensor_scalar(
-                    live[e][:, h, :, :], a_sb[e][:, h, :, :].rearrange("p d c -> p c d"), 0.0, None, IS_GT
-                )
+        def make_mask(e, where):
+            live[e] = where.rearrange("p (h c d) -> p h c d", h=HALVES, d=4)
+            nc.vector.tensor_scalar(live[e], a_sb[e][:].rearrange("p h d c -> p h c d"), 0.0, None, IS_GT)
 
-        def mask(q):
+        def mask(q, da):
             e, lo = q * P // C, q * P % C
-            das[q] = work.tile([P, HALVES, P, 4], BF16, name="da", align_bytes=64)
+            das[q] = da
             nc.vector.tensor_tensor(
-                das[q][:].rearrange("p h c d -> p h (c d)"),
+                da.rearrange("p (h x) -> p h x", h=HALVES),
                 xts[q][:].rearrange("p h c u -> p h (c u)").bitcast(BF16),
                 live[e][:, :, lo : lo + P, :].rearrange("p h c d -> p h (c d)"),
                 MULT,
@@ -167,9 +169,7 @@ def tile_moe_bdx_mlp_relu_kernel(
         def quantize_da(q):
             codes = work.tile([P, HALVES * P], U32, name="da_codes", align_bytes=64)
             scales = work.tile([P, HALVES * P], U8, name="da_scales", align_bytes=64)
-            nc.vector.quantize_mx(
-                out=codes[:].bitcast(E4M3), scales=scales[:], in_=das[q][:].rearrange("p h c d -> p (h c d)")
-            )
+            nc.vector.quantize_mx(out=codes[:].bitcast(E4M3), scales=scales[:], in_=das[q])
             codes2[q] = codes, scales
 
         def multiply_w1(q, dx_sb):
@@ -192,46 +192,60 @@ def tile_moe_bdx_mlp_relu_kernel(
         def scatter(lo, n, dx_sb):
             nc.vector.tensor_copy(window[:].indirect(offsets[:, lo // 16 : (lo + n) // 16]), dx_sb)
 
-        every = range(PASSES)
-        gather(0, 0, C)
-        gather(1, 0, C)
-        quantize_g(0, 0, C)
-        gather(2, 0, C)
-        quantize_g(1, 0, C)
-        gather(0, C, C)
-        quantize_g(2, 0, C)
-        multiply_w2(0, every)
-        multiply_w2(1, every)
-        gather(1, C, C)
+        staged = held.tile([P, 8 * C], BF16, name="staged", align_bytes=64)
+        reused = held.tile([P, 12 * C], BF16, name="reused", align_bytes=64)
+        da2 = held.tile([P, 4 * C], BF16, name="da2", align_bytes=64)
+        da3 = held.tile([P, 4 * C], BF16, name="da3", align_bytes=64)
+        dx01 = held.tile([P, C], F32, name="dx01")
+        dx2 = held.tile([P, P], F32, name="dx2")
+        dx3 = held.tile([P, P], F32, name="dx3")
+
+        gather(0, 0)
+        interleave(0, 0)
+        gather(1, 0)
+        interleave(1, 0)
+        quantize_g(0, 0)
+        gather(2, 0)
+        interleave(2, 0)
+        quantize_g(1, 0)
+        gather(0, 1, "gate_sb0")
+        interleave(0, 1)
+        quantize_g(2, 0)
+        multiply_w2(0, (0, 1))
+        multiply_w2(1, (0, 1))
+        multiply_w2(0, (2,))
+        multiply_w2(1, (2,))
         turn(0)
-        gather(2, C, C)
-        turn(1)
-        quantize_g(0, C, C)
-        quantize_g(1, C, C)
-        multiply_w2(2, (0, 1))
-        multiply_w2(3, (0, 1))
-        make_mask(0)
-        mask(0)
-        quantize_g(2, C, C)
+        turn(1, (staged[:, 0 : 2 * C], reused[:, 6 * C : 8 * C]))
+        gather(1, 1, "wide2_0")
+        interleave(1, 1, staged[:, 0 : 4 * C])
+        quantize_g(0, 1)
+        gather(2, 1, "wide0_1")
+        interleave(2, 1, reused[:, 6 * C : 10 * C])
+        quantize_g(1, 1)
+        multiply_w2(2, (0,))
+        multiply_w2(3, (0,))
+        multiply_w2(2, (1,))
+        multiply_w2(3, (1,))
+        make_mask(0, staged[:])
+        quantize_g(2, 1, "a_sb0")
         multiply_w2(2, (2,))
         multiply_w2(3, (2,))
-        mask(1)
-        dx01 = held.tile([P, C], F32, name="dx01")
+        mask(0, reused[:, 4 * C : 8 * C])
+        mask(1, reused[:, 8 * C : 12 * C])
         quantize_da(0)
-        multiply_w1(0, dx01[:, 0:P])
         quantize_da(1)
-        multiply_w1(1, dx01[:, P:C])
         turn(2)
-        make_mask(1)
         turn(3)
+        multiply_w1(0, dx01[:, 0:P])
+        multiply_w1(1, dx01[:, P:C])
+        make_mask(1, reused[:, 0 : 8 * C])
         scatter(0, C, dx01[:])
-        mask(2)
-        mask(3)
+        mask(2, da2[:])
         quantize_da(2)
-        dx2 = held.tile([P, P], F32, name="dx2")
         multiply_w1(2, dx2[:])
+        mask(3, da3[:])
         quantize_da(3)
-        dx3 = held.tile([P, P], F32, name="dx3")
         multiply_w1(3, dx3[:])
         scatter(C, P, dx2[:])
         scatter(C + P, P, dx3[:])

@@ -32,119 +32,104 @@ def tile_moe_bdx_mlp_relu_kernel(
     with ExitStack() as ctx:
         held = ctx.enter_context(tc.tile_pool(name="held", bufs=1))
         work = ctx.enter_context(tc.tile_pool(name="work", bufs=3))
-        dh_pool = ctx.enter_context(tc.psum_pool(name="dh_pool", bufs=4))
-        xt_pool = ctx.enter_context(tc.psum_pool(name="xt_pool", bufs=2))
-        o_pool = ctx.enter_context(tc.psum_pool(name="o_pool", bufs=2))
+        banks = ctx.enter_context(tc.psum_pool(name="banks", bufs=8))
 
         offsets = held.tile([P, S // 16], U16, name="offsets")
         nc.sync.dma_start(offsets[:], offs)
 
-        gate_sb = [held.tile([P, C], F32, name=f"gate_sb{e}", align_bytes=64) for e in range(E)]
+        gate_sb = held.tile([P, S], F32, name="gate_sb")
+        gate_first = held.tile([P, C], F32, name="gate_first", align_bytes=64)
         w2_planes = held.tile([P, E * PASSES, H], U8, name="w2_planes", align_bytes=64)
         w1_planes = held.tile([P, E * HALVES, K], U8, name="w1_planes", align_bytes=64)
         window = held.tile([P, T], F32, name="window")
         identity = held.tile([P, P], F32, name="identity")
-        nc.gpsimd.memset(w2_planes[:].rearrange("p n c -> p (n c)").bitcast(I32), 0)
-        nc.gpsimd.memset(w1_planes[:].rearrange("p n c -> p (n c)").bitcast(I32), 0)
+        nc.vector.memset(w2_planes[:].rearrange("p n c -> p (n c)").bitcast(I32), 0)
+        nc.vector.memset(w1_planes[:].rearrange("p n c -> p (n c)").bitcast(I32), 0)
+        nc.vector.memset(window[:], 0.0)
         make_identity(nc, identity[:])
-        nc.gpsimd.memset(window[:], 0.0)
 
         dy_view = dyT.rearrange("(s p d) t -> s d p t", p=P, d=4)
         dy = [[held.tile([P, T], F32, name=f"dy{s}_{d}") for d in range(4)] for s in range(PASSES)]
-        w2_sb = [held.tile([P, PASSES, 2 * H], U8, name=f"w2_sb{e}", align_bytes=64) for e in range(E)]
+        w2_sb = [held.tile([P, E, 2 * H], U8, name=f"w2_sb{s}", align_bytes=64) for s in range(PASSES)]
         w1_sb = held.tile([P, E * HALVES, 2 * K], U8, name="w1_sb", align_bytes=64)
-        a_sb = [held.tile([P, HALVES, 4, C], F32, name=f"a_sb{e}", align_bytes=64) for e in range(E)]
-        a_view = a.rearrange("(h p d) c -> h p d c", p=P, d=4)
+        a_sb = [held.tile([P, 4 * S], F32, name=f"a_sb{h}", align_bytes=64) for h in range(HALVES)]
+        a_view = a.rearrange("(h p d) c -> h p (d c)", p=P, d=4)
 
         def load_dy(s):
             for d in range(4):
                 nc.sync.dma_start(dy[s][d][:], dy_view[s, d])
 
-        def load_gate(e):
-            nc.sync.dma_start(gate_sb[e][:], gate[0:P, e * C : (e + 1) * C])
-
-        def load_w2(e):
-            nc.sync.dma_start(w2_sb[e][:].bitcast(I32), w2_words[e].rearrange("s p c -> p s c").bitcast(I32))
-
-        def load_a(e):
-            for h in range(HALVES):
-                nc.sync.dma_start(a_sb[e][:, h, :, :], a_view[h, :, :, e * C : (e + 1) * C])
+        def load_w2(s):
+            nc.sync.dma_start(w2_sb[s][:].bitcast(I32), w2_words[:, s].rearrange("e p c -> p e c").bitcast(I32))
 
         def load_scales(planes, scales):
-            by_pass = scales.rearrange("e s f c -> (e s) f c")
-            for quad in range(4):
-                nc.sync.dma_start(
-                    planes[32 * quad : 32 * quad + 4, :, :].bitcast(I32),
-                    by_pass[:, 4 * quad : 4 * quad + 4, :].rearrange("n r c -> r n c").bitcast(I32),
-                )
+            by_row = scales.rearrange("e s (quad r) c -> r quad (e s) c", r=4)
+            for r in range(4):
+                nc.sync.dma_start(planes[r:P:32, :, :].bitcast(I32), by_row[r].bitcast(I32))
 
-        load_gate(0)
+        nc.sync.dma_start(gate_sb[:], gate[0:P, :])
         load_dy(0)
         load_dy(1)
-        load_dy(2)
-        load_gate(1)
-        load_w2(0)
         load_scales(w2_planes, w2_scales)
-        load_scales(w1_planes, w1_scales)
-        load_a(0)
-        load_w2(1)
+        load_dy(2)
+        for s in range(PASSES):
+            load_w2(s)
+        for h in range(HALVES):
+            nc.sync.dma_start(a_sb[h][:], a_view[h])
         nc.sync.dma_start(w1_sb[:].bitcast(I32), w1_words.rearrange("e s p c -> p (e s) c").bitcast(I32))
-        load_a(1)
+        load_scales(w1_planes, w1_scales)
+        nc.scalar.copy(gate_first[:], gate_sb[:, 0:C])
 
-        g, g_wide, g_codes, g_scales = {}, {}, {}, {}
+        g_codes, g_scales = {}, {}
 
-        def gather(s, e, tag=None):
-            g[s, e] = held.tile([P, 4 * C], F32, name=f"g{s}_{e}", tag=tag or f"g{s}_{e}", align_bytes=64)[:]
+        def gather(s, lo, n, gates, g):
             for d in range(4):
                 nc.vector.tensor_tensor(
-                    g[s, e][:, d * C : (d + 1) * C],
-                    dy[s][d][:].indirect(offsets[:, e * C // 16 : (e + 1) * C // 16]),
-                    gate_sb[e][:],
+                    g[:, d * n : (d + 1) * n],
+                    dy[s][d][:].indirect(offsets[:, lo // 16 : (lo + n) // 16]),
+                    gates,
                     MULT,
                 )
 
-        def interleave(s, e, wide=None):
-            if wide is None:
-                wide = held.tile([P, 4 * C], BF16, name=f"wide{s}_{e}", align_bytes=64)[:]
-            nc.scalar.copy(
-                wide.rearrange("p (c i d) -> p c d i", i=4, d=4), g[s, e].rearrange("p (d c i) -> p c d i", i=4, d=4)
-            )
-            g_wide[s, e] = wide
+        def interleave(wide, g):
+            nc.scalar.copy(wide.rearrange("p (c i d) -> p c d i", i=4, d=4), g.rearrange("p (d c i) -> p c d i", i=4, d=4))
 
-        def quantize_g(s, e, tag=None):
-            codes = held.tile([P, C], U32, name=f"g_codes{s}_{e}", tag=tag or f"g_codes{s}_{e}", align_bytes=64)
-            scales = held.tile([P, C], U8, name=f"g_scales{s}_{e}", align_bytes=64)
-            nc.vector.quantize_mx(out=codes[:].bitcast(E4M3), scales=scales[:], in_=g_wide[s, e])
-            for q in range(2 * e, 2 * e + 2):
-                cols = slice(q * P - e * C, q * P - e * C + P)
+        def quantize_g(s, lo, n, wide, tag=None):
+            codes = held.tile([P, n], U32, name=f"g_codes{s}_{lo}", tag=tag or f"g_codes{s}_{lo}", align_bytes=64)
+            scales = held.tile([P, n], U8, name=f"g_scales{s}_{lo}", align_bytes=64)
+            nc.vector.quantize_mx(out=codes[:].bitcast(E4M3), scales=scales[:], in_=wide)
+            for q in range(lo // P, (lo + n) // P):
+                cols = slice(q * P - lo, q * P - lo + P)
                 g_codes[s, q] = codes[:, cols]
                 g_scales[s, q] = scales[:, cols]
 
-        dh, xts, live, das, codes2 = {}, {}, {}, {}, {}
+        dh, xts, das, codes2, staged = {}, {}, {}, {}, {}
 
         def multiply_w2(q, passes):
             e = q * P // C
             for h in range(HALVES):
                 if 0 in passes:
-                    dh[q, h] = dh_pool.tile([P, 512], F32, name="dh")
+                    dh[q, h] = banks.tile([P, 512], F32, name="dh", tag="bank")
                 for s in passes:
                     nc.tensor.matmul_mx(
                         out=dh[q, h][:],
                         lhsT=g_codes[s, q].bitcast(E4M3),
                         lhsT_scale=g_scales[s, q],
-                        rhs=w2_sb[e][:, s, 1024 * h : 1024 * (h + 1)].bitcast(E2M1),
+                        rhs=w2_sb[s][:, e, 1024 * h : 1024 * (h + 1)].bitcast(E2M1),
                         rhs_scale=w2_planes[:, e * PASSES + s, 512 * h : 512 * (h + 1)],
                         start=(s == 0),
                         stop=(s == PASSES - 1),
                     )
 
-        def turn(q, staging=None):
-            xts[q] = xt_pool.tile([P, HALVES, P, 2], F32, name="xt")
+        def turn(q):
+            xts[q] = banks.tile([P, HALVES, P, 2], F32, name="xt", tag="bank")
             for h in range(HALVES):
-                if staging is None:
-                    dhb = work.tile([P, 512], BF16, name="dhb")[:]
+                place = HALVES * q + h - 1
+                if not 0 <= place < 3:
+                    dhb = held.tile([P, 512], BF16, name=f"dhb{q}_{h}")[:]
+                    staged[q, h] = dhb
                 else:
-                    dhb = staging[h]
+                    dhb = staging[:, 512 * place : 512 * (place + 1)]
                 nc.scalar.copy(
                     dhb.rearrange("c (u p b) -> c u p b", u=2, b=2),
                     dh[q, h][:].rearrange("c (p u b) -> c u p b", u=2, b=2),
@@ -152,30 +137,34 @@ def tile_moe_bdx_mlp_relu_kernel(
                 for u in range(2):
                     nc.tensor.transpose(xts[q][:, h, :, u], dhb[:, 256 * u : 256 * (u + 1)].bitcast(F32), identity[:])
 
-        def make_mask(e, where):
-            live[e] = where.rearrange("p (h c d) -> p h c d", h=HALVES, d=4)
-            nc.vector.tensor_scalar(live[e], a_sb[e][:].rearrange("p h d c -> p h c d"), 0.0, None, IS_GT)
+        def make_mask(h):
+            nc.vector.tensor_scalar(
+                live[:, h, :].rearrange("p (c i d) -> p c d i", i=4, d=4),
+                a_sb[h][:].rearrange("p (d c i) -> p c d i", i=4, d=4),
+                0.0,
+                None,
+                IS_GT,
+            )
 
-        def mask(q, da):
-            e, lo = q * P // C, q * P % C
-            das[q] = da
+        def mask(q):
+            das[q] = held.tile([P, HALVES * 512], BF16, name=f"da{q}", align_bytes=64)
             nc.vector.tensor_tensor(
-                da.rearrange("p (h x) -> p h x", h=HALVES),
+                das[q][:].rearrange("p (h x) -> p h x", h=HALVES),
                 xts[q][:].rearrange("p h c u -> p h (c u)").bitcast(BF16),
-                live[e][:, :, lo : lo + P, :].rearrange("p h c d -> p h (c d)"),
+                live[:, :, 512 * q : 512 * (q + 1)],
                 MULT,
             )
 
         def quantize_da(q):
             codes = work.tile([P, HALVES * P], U32, name="da_codes", align_bytes=64)
             scales = work.tile([P, HALVES * P], U8, name="da_scales", align_bytes=64)
-            nc.vector.quantize_mx(out=codes[:].bitcast(E4M3), scales=scales[:], in_=das[q])
+            nc.vector.quantize_mx(out=codes[:].bitcast(E4M3), scales=scales[:], in_=das[q][:])
             codes2[q] = codes, scales
 
         def multiply_w1(q, dx_sb):
             e = q * P // C
             codes, scales = codes2[q]
-            dx = o_pool.tile([P, P], F32, name="dx")
+            dx = banks.tile([P, P], F32, name="dx", tag="bank")
             for h in range(HALVES):
                 cols = slice(h * P, (h + 1) * P)
                 nc.tensor.matmul_mx(
@@ -192,59 +181,56 @@ def tile_moe_bdx_mlp_relu_kernel(
         def scatter(lo, n, dx_sb):
             nc.vector.tensor_copy(window[:].indirect(offsets[:, lo // 16 : (lo + n) // 16]), dx_sb)
 
-        staged = held.tile([P, 8 * C], BF16, name="staged", align_bytes=64)
-        reused = held.tile([P, 12 * C], BF16, name="reused", align_bytes=64)
-        da2 = held.tile([P, 4 * C], BF16, name="da2", align_bytes=64)
-        da3 = held.tile([P, 4 * C], BF16, name="da3", align_bytes=64)
         dx01 = held.tile([P, C], F32, name="dx01")
         dx2 = held.tile([P, P], F32, name="dx2")
         dx3 = held.tile([P, P], F32, name="dx3")
+        g_all = [held.tile([P, 4 * S], F32, name=f"g_all{s}") for s in range(2)]
+        wide_all = [held.tile([P, 4 * S], BF16, name=f"wide_all{s}", align_bytes=64) for s in range(2)]
+        g_first = held.tile([P, 4 * C], F32, name="g_first")
+        staging = held.tile([P, 3 * 512], BF16, name="staging", align_bytes=64)
+        wide_last = staging[:, C : 5 * C]
 
-        gather(0, 0)
-        interleave(0, 0)
-        gather(1, 0)
-        interleave(1, 0)
-        quantize_g(0, 0)
-        gather(2, 0)
-        interleave(2, 0)
-        quantize_g(1, 0)
-        gather(0, 1, "gate_sb0")
-        interleave(0, 1)
-        quantize_g(2, 0)
-        multiply_w2(0, (0, 1))
-        multiply_w2(1, (0, 1))
-        multiply_w2(0, (2,))
-        multiply_w2(1, (2,))
-        turn(0)
-        turn(1, (staged[:, 0 : 2 * C], reused[:, 6 * C : 8 * C]))
-        gather(1, 1, "wide2_0")
-        interleave(1, 1, staged[:, 0 : 4 * C])
-        quantize_g(0, 1)
-        gather(2, 1, "wide0_1")
-        interleave(2, 1, reused[:, 6 * C : 10 * C])
-        quantize_g(1, 1)
-        multiply_w2(2, (0,))
-        multiply_w2(3, (0,))
+        gather(0, 0, S, gate_sb[:], g_all[0][:])
+        interleave(wide_all[0][:], g_all[0][:])
+        gather(1, 0, S, gate_sb[:], g_all[1][:])
+        interleave(wide_all[1][:], g_all[1][:])
+        quantize_g(0, 0, S, wide_all[0][:])
+        gather(2, 0, C, gate_first[:], g_first[:])
+        quantize_g(1, 0, S, wide_all[1][:], "gate_first")
+        late = held.tile([P, 5 * C], F32, name="late", tag="wide_all1", align_bytes=64)
+        wide_first = late[:, 3 * C : 5 * C].bitcast(BF16)
+        interleave(wide_first, g_first[:])
+        quantize_g(2, 0, C, wide_first)
+        gather(2, C, C, gate_sb[:, C:S], late[:, 0 : 4 * C])
+        interleave(wide_last, late[:, 0 : 4 * C])
+        for q in range(GROUPS):
+            multiply_w2(q, (0,))
+        for s in (1, 2):
+            multiply_w2(0, (s,))
+            multiply_w2(1, (s,))
         multiply_w2(2, (1,))
         multiply_w2(3, (1,))
-        make_mask(0, staged[:])
-        quantize_g(2, 1, "a_sb0")
+        live = held.tile([P, HALVES, 4 * S], BF16, name="live", tag="dy2_2")
+        make_mask(0)
+        quantize_g(2, C, C, wide_last, "a_sb0")
         multiply_w2(2, (2,))
         multiply_w2(3, (2,))
-        mask(0, reused[:, 4 * C : 8 * C])
-        mask(1, reused[:, 8 * C : 12 * C])
-        quantize_da(0)
-        quantize_da(1)
+        turn(0)
+        turn(1)
+        make_mask(1)
         turn(2)
         turn(3)
+        mask(0)
+        mask(1)
+        quantize_da(0)
+        quantize_da(1)
         multiply_w1(0, dx01[:, 0:P])
         multiply_w1(1, dx01[:, P:C])
-        make_mask(1, reused[:, 0 : 8 * C])
+        mask(2)
         scatter(0, C, dx01[:])
-        mask(2, da2[:])
         quantize_da(2)
         multiply_w1(2, dx2[:])
-        mask(3, da3[:])
+        mask(3)
         quantize_da(3)
         multiply_w1(3, dx3[:])
         scatter(C, P, dx2[:])

@@ -49,50 +49,55 @@ def tile_moe_bdx_mlp_relu_kernel(
         make_identity(nc, identity[:])
 
         dy_view = dyT.rearrange("(s p d) t -> s d p t", p=P, d=4)
-        dy = [[held.tile([P, T], F32, name=f"dy{s}_{d}") for d in range(4)] for s in range(PASSES)]
-        w2_sb = [held.tile([P, E, 2 * H], U8, name=f"w2_sb{s}", align_bytes=64) for s in range(PASSES)]
+        dy = [[held.tile([P, T], F32, name=f"dy{s}_{d}", align_bytes=64) for d in range(4)] for s in range(PASSES)]
+        w2_sb = [held.tile([P, PASSES, 2 * H], U8, name=f"w2_sb{e}", align_bytes=64) for e in range(E)]
         w1_sb = held.tile([P, E * HALVES, 2 * K], U8, name="w1_sb", align_bytes=64)
-        a_sb = [held.tile([P, 4 * S], F32, name=f"a_sb{h}", align_bytes=64) for h in range(HALVES)]
-        a_view = a.rearrange("(h p d) c -> h p (d c)", p=P, d=4)
+        a_sb = [[held.tile([P, 4, C], F32, name=f"a_sb{e}_{h}", align_bytes=64) for h in range(HALVES)] for e in range(E)]
+        a_view = a.rearrange("(h p d) (e c) -> e h p d c", p=P, d=4, e=E)
 
-        def load_dy(s):
-            for d in range(4):
+        def load_dy(s, rows=range(4)):
+            for d in rows:
                 nc.sync.dma_start(dy[s][d][:], dy_view[s, d])
 
-        def load_w2(s):
-            nc.sync.dma_start(w2_sb[s][:].bitcast(I32), w2_words[:, s].rearrange("e p c -> p e c").bitcast(I32))
+        def load_w2(e):
+            nc.sync.dma_start(w2_sb[e][:].bitcast(I32), w2_words[e].rearrange("s p c -> p s c").bitcast(I32))
+
+        def load_a(e):
+            for h in range(HALVES):
+                nc.sync.dma_start(a_sb[e][h][:], a_view[e, h])
 
         def load_scales(planes, scales):
             by_row = scales.rearrange("e s (quad r) c -> r quad (e s) c", r=4)
             for r in range(4):
                 nc.sync.dma_start(planes[r:P:32, :, :].bitcast(I32), by_row[r].bitcast(I32))
 
-        nc.sync.dma_start(gate_sb[:], gate[0:P, :])
-        load_dy(0)
+        nc.sync.dma_start(gate_sb[:, 0:C], gate[0:P, 0:C])
+        load_dy(0, (0,))
+        nc.sync.dma_start(gate_sb[:, C:S], gate[0:P, C:S])
+        load_dy(0, (1, 2, 3))
         load_dy(1)
         load_scales(w2_planes, w2_scales)
         load_dy(2)
-        for s in range(PASSES):
-            load_w2(s)
-        for h in range(HALVES):
-            nc.sync.dma_start(a_sb[h][:], a_view[h])
+        for e in range(E):
+            load_w2(e)
+        load_a(0)
+        load_a(1)
         nc.sync.dma_start(w1_sb[:].bitcast(I32), w1_words.rearrange("e s p c -> p (e s) c").bitcast(I32))
         load_scales(w1_planes, w1_scales)
         nc.scalar.copy(gate_first[:], gate_sb[:, 0:C])
 
         g_codes, g_scales = {}, {}
 
-        def gather(s, lo, n, gates, g):
-            for d in range(4):
-                nc.vector.tensor_tensor(
-                    g[:, d * n : (d + 1) * n],
-                    dy[s][d][:].indirect(offsets[:, lo // 16 : (lo + n) // 16]),
-                    gates,
-                    MULT,
-                )
+        def gather_row(s, d, lo, n, gates, g_row):
+            nc.vector.tensor_tensor(g_row, dy[s][d][:].indirect(offsets[:, lo // 16 : (lo + n) // 16]), gates, MULT)
 
-        def interleave(wide, g):
-            nc.scalar.copy(wide.rearrange("p (c i d) -> p c d i", i=4, d=4), g.rearrange("p (d c i) -> p c d i", i=4, d=4))
+        def gather(s, lo, n, gates, g, rows=range(4)):
+            for d in rows:
+                gather_row(s, d, lo, n, gates, g[:, d * n : (d + 1) * n])
+
+        def interleave(wide, g, cols=slice(None)):
+            rows = g.rearrange("p (d c) -> p d c", d=4)[:, :, cols]
+            nc.scalar.copy(wide.rearrange("p (c i d) -> p c d i", i=4, d=4), rows.rearrange("p d (c i) -> p c d i", i=4))
 
         def quantize_g(s, lo, n, wide, tag=None):
             codes = held.tile([P, n], U32, name=f"g_codes{s}_{lo}", tag=tag or f"g_codes{s}_{lo}", align_bytes=64)
@@ -103,7 +108,7 @@ def tile_moe_bdx_mlp_relu_kernel(
                 g_codes[s, q] = codes[:, cols]
                 g_scales[s, q] = scales[:, cols]
 
-        dh, xts, das, codes2, staged = {}, {}, {}, {}, {}
+        dh, xts, das, codes2, staged, live = {}, {}, {}, {}, {}, {}
 
         def multiply_w2(q, passes):
             e = q * P // C
@@ -115,7 +120,7 @@ def tile_moe_bdx_mlp_relu_kernel(
                         out=dh[q, h][:],
                         lhsT=g_codes[s, q].bitcast(E4M3),
                         lhsT_scale=g_scales[s, q],
-                        rhs=w2_sb[s][:, e, 1024 * h : 1024 * (h + 1)].bitcast(E2M1),
+                        rhs=w2_sb[e][:, s, 1024 * h : 1024 * (h + 1)].bitcast(E2M1),
                         rhs_scale=w2_planes[:, e * PASSES + s, 512 * h : 512 * (h + 1)],
                         start=(s == 0),
                         stop=(s == PASSES - 1),
@@ -124,12 +129,11 @@ def tile_moe_bdx_mlp_relu_kernel(
         def turn(q):
             xts[q] = banks.tile([P, HALVES, P, 2], F32, name="xt", tag="bank")
             for h in range(HALVES):
-                place = HALVES * q + h - 1
-                if not 0 <= place < 3:
+                if (q, h) not in ((0, 0), (1, 1)):
                     dhb = held.tile([P, 512], BF16, name=f"dhb{q}_{h}")[:]
                     staged[q, h] = dhb
                 else:
-                    dhb = staging[:, 512 * place : 512 * (place + 1)]
+                    dhb = wide_last[:, 0:512]
                 nc.scalar.copy(
                     dhb.rearrange("c (u p b) -> c u p b", u=2, b=2),
                     dh[q, h][:].rearrange("c (p u b) -> c u p b", u=2, b=2),
@@ -137,21 +141,23 @@ def tile_moe_bdx_mlp_relu_kernel(
                 for u in range(2):
                     nc.tensor.transpose(xts[q][:, h, :, u], dhb[:, 256 * u : 256 * (u + 1)].bitcast(F32), identity[:])
 
-        def make_mask(h):
-            nc.vector.tensor_scalar(
-                live[:, h, :].rearrange("p (c i d) -> p c d i", i=4, d=4),
-                a_sb[h][:].rearrange("p (d c i) -> p c d i", i=4, d=4),
-                0.0,
-                None,
-                IS_GT,
-            )
+        def make_mask(e, tag):
+            live[e] = held.tile([P, HALVES, 4 * C], BF16, name=f"live{e}", tag=tag, align_bytes=64)
+            for h in range(HALVES):
+                nc.vector.tensor_scalar(
+                    live[e][:, h, :].rearrange("p (c i d) -> p c d i", i=4, d=4),
+                    a_sb[e][h][:].rearrange("p d (c i) -> p c d i", i=4),
+                    0.0,
+                    None,
+                    IS_GT,
+                )
 
         def mask(q):
             das[q] = held.tile([P, HALVES * 512], BF16, name=f"da{q}", align_bytes=64)
             nc.vector.tensor_tensor(
                 das[q][:].rearrange("p (h x) -> p h x", h=HALVES),
                 xts[q][:].rearrange("p h c u -> p h (c u)").bitcast(BF16),
-                live[:, :, 512 * q : 512 * (q + 1)],
+                live[q // 2][:, :, 512 * (q % 2) : 512 * (q % 2 + 1)],
                 MULT,
             )
 
@@ -181,58 +187,61 @@ def tile_moe_bdx_mlp_relu_kernel(
         def scatter(lo, n, dx_sb):
             nc.vector.tensor_copy(window[:].indirect(offsets[:, lo // 16 : (lo + n) // 16]), dx_sb)
 
-        dx01 = held.tile([P, C], F32, name="dx01")
-        dx2 = held.tile([P, P], F32, name="dx2")
+        dx012 = held.tile([P, 3 * P], F32, name="dx012")
         dx3 = held.tile([P, P], F32, name="dx3")
         g_all = [held.tile([P, 4 * S], F32, name=f"g_all{s}") for s in range(2)]
-        wide_all = [held.tile([P, 4 * S], BF16, name=f"wide_all{s}", align_bytes=64) for s in range(2)]
+        wide_zero = held.tile([P, 4 * S], BF16, name="wide_zero", align_bytes=64)
         g_first = held.tile([P, 4 * C], F32, name="g_first")
-        staging = held.tile([P, 3 * 512], BF16, name="staging", align_bytes=64)
-        wide_last = staging[:, C : 5 * C]
+        wide_last = held.tile([P, 4 * C], BF16, name="wide_last", align_bytes=64)
+        wide_one = held.tile([P, 4 * C], BF16, name="wide_one", align_bytes=64)
+        g_last = held.tile([P, 4 * C], F32, name="g_last", align_bytes=64)
+        wide_mid = g_last[:, 0 : 2 * C].bitcast(BF16)
+        wide_first = g_last[:, 2 * C : 4 * C].bitcast(BF16)
 
-        gather(0, 0, S, gate_sb[:], g_all[0][:])
-        interleave(wide_all[0][:], g_all[0][:])
+        for lo in (0, C):
+            gather_row(0, 0, lo, C, gate_sb[:, lo : lo + C], g_all[0][:, lo : lo + C])
+        gather(0, 0, S, gate_sb[:], g_all[0][:], (1, 2, 3))
+        interleave(wide_zero[:], g_all[0][:])
         gather(1, 0, S, gate_sb[:], g_all[1][:])
-        interleave(wide_all[1][:], g_all[1][:])
-        quantize_g(0, 0, S, wide_all[0][:])
+        interleave(wide_mid, g_all[1][:], slice(0, C))
+        interleave(wide_one[:], g_all[1][:], slice(C, S))
+        quantize_g(0, 0, C, wide_zero[:, 0 : 4 * C])
         gather(2, 0, C, gate_first[:], g_first[:])
-        quantize_g(1, 0, S, wide_all[1][:], "gate_first")
-        late = held.tile([P, 5 * C], F32, name="late", tag="wide_all1", align_bytes=64)
-        wide_first = late[:, 3 * C : 5 * C].bitcast(BF16)
         interleave(wide_first, g_first[:])
+        quantize_g(1, 0, C, wide_mid, "gate_first")
         quantize_g(2, 0, C, wide_first)
-        gather(2, C, C, gate_sb[:, C:S], late[:, 0 : 4 * C])
-        interleave(wide_last, late[:, 0 : 4 * C])
-        for q in range(GROUPS):
-            multiply_w2(q, (0,))
-        for s in (1, 2):
+        gather(2, C, C, gate_sb[:, C:S], g_last[:])
+        for s in range(PASSES):
             multiply_w2(0, (s,))
             multiply_w2(1, (s,))
+        turn(0)
+        interleave(wide_last[:], g_last[:])
+        quantize_g(0, C, C, wide_zero[:, 4 * C : 8 * C], "dy2_2")
+        multiply_w2(2, (0,))
+        multiply_w2(3, (0,))
+        make_mask(0, "dy2_3")
+        quantize_g(1, C, C, wide_one[:], "a_sb0_1")
         multiply_w2(2, (1,))
         multiply_w2(3, (1,))
-        live = held.tile([P, HALVES, 4 * S], BF16, name="live", tag="dy2_2")
-        make_mask(0)
-        quantize_g(2, C, C, wide_last, "a_sb0")
+        mask(0)
+        quantize_g(2, C, C, wide_last[:], "wide_one")
         multiply_w2(2, (2,))
         multiply_w2(3, (2,))
-        turn(0)
         turn(1)
-        make_mask(1)
         turn(2)
         turn(3)
-        mask(0)
-        mask(1)
         quantize_da(0)
+        mask(1)
         quantize_da(1)
-        multiply_w1(0, dx01[:, 0:P])
-        multiply_w1(1, dx01[:, P:C])
+        make_mask(1, "live1")
+        multiply_w1(0, dx012[:, 0:P])
+        multiply_w1(1, dx012[:, P:C])
         mask(2)
-        scatter(0, C, dx01[:])
         quantize_da(2)
-        multiply_w1(2, dx2[:])
+        multiply_w1(2, dx012[:, C : 3 * P])
         mask(3)
         quantize_da(3)
         multiply_w1(3, dx3[:])
-        scatter(C, P, dx2[:])
+        scatter(0, 3 * P, dx012[:])
         scatter(C + P, P, dx3[:])
         nc.sync.dma_start(out, window[:])

@@ -31,14 +31,12 @@ def tile_moe_bdx_mlp_relu_kernel(
     nc = tc.nc
     with ExitStack() as ctx:
         held = ctx.enter_context(tc.tile_pool(name="held", bufs=1))
-        work = ctx.enter_context(tc.tile_pool(name="work", bufs=3))
         banks = ctx.enter_context(tc.psum_pool(name="banks", bufs=8))
 
         offsets = held.tile([P, S // 16], U16, name="offsets")
-        nc.sync.dma_start(offsets[:], offs)
 
         gate_sb = held.tile([P, S], F32, name="gate_sb")
-        gate_first = held.tile([P, C], F32, name="gate_first", align_bytes=64)
+        gate_pair = [held.tile([P, C], F32, name=f"gate_pair{i}", align_bytes=64) for i in range(2)]
         w2_planes = held.tile([P, E * PASSES, H], U8, name="w2_planes", align_bytes=64)
         w1_planes = held.tile([P, E * HALVES, K], U8, name="w1_planes", align_bytes=64)
         window = held.tile([P, T], F32, name="window")
@@ -50,7 +48,9 @@ def tile_moe_bdx_mlp_relu_kernel(
 
         dy_view = dyT.rearrange("(s p d) t -> s d p t", p=P, d=4)
         dy = [[held.tile([P, T], F32, name=f"dy{s}_{d}", align_bytes=64) for d in range(4)] for s in range(PASSES)]
-        w2_sb = [held.tile([P, PASSES, 2 * H], U8, name=f"w2_sb{e}", align_bytes=64) for e in range(E)]
+        w2_zero = held.tile([P, E, 2 * H], U8, name="w2_zero", align_bytes=64)
+        w2_rest = [held.tile([P, PASSES - 1, 2 * H], U8, name=f"w2_rest{e}", align_bytes=64) for e in range(E)]
+        w2_sb = [[w2_zero[:, e, :], w2_rest[e][:, 0, :], w2_rest[e][:, 1, :]] for e in range(E)]
         w1_sb = held.tile([P, E * HALVES, 2 * K], U8, name="w1_sb", align_bytes=64)
         a_sb = [[held.tile([P, 4, C], F32, name=f"a_sb{e}_{h}", align_bytes=64) for h in range(HALVES)] for e in range(E)]
         a_view = a.rearrange("(h p d) (e c) -> e h p d c", p=P, d=4, e=E)
@@ -60,7 +60,7 @@ def tile_moe_bdx_mlp_relu_kernel(
                 nc.sync.dma_start(dy[s][d][:], dy_view[s, d])
 
         def load_w2(e):
-            nc.sync.dma_start(w2_sb[e][:].bitcast(I32), w2_words[e].rearrange("s p c -> p s c").bitcast(I32))
+            nc.sync.dma_start(w2_rest[e][:].bitcast(I32), w2_words[e, 1:].rearrange("s p c -> p s c").bitcast(I32))
 
         def load_a(e):
             for h in range(HALVES):
@@ -71,20 +71,23 @@ def tile_moe_bdx_mlp_relu_kernel(
             for r in range(4):
                 nc.sync.dma_start(planes[r:P:32, :, :].bitcast(I32), by_row[r].bitcast(I32))
 
-        nc.sync.dma_start(gate_sb[:, 0:C], gate[0:P, 0:C])
         load_dy(0, (0,))
+        nc.sync.dma_start(gate_sb[:, 0:C], gate[0:P, 0:C])
+        nc.sync.dma_start(offsets[:], offs)
         nc.sync.dma_start(gate_sb[:, C:S], gate[0:P, C:S])
         load_dy(0, (1, 2, 3))
         load_dy(1)
         load_scales(w2_planes, w2_scales)
         load_dy(2)
+        nc.sync.dma_start(w2_zero[:].bitcast(I32), w2_words[:, 0].rearrange("e p c -> p e c").bitcast(I32))
         for e in range(E):
             load_w2(e)
         load_a(0)
         load_a(1)
         nc.sync.dma_start(w1_sb[:].bitcast(I32), w1_words.rearrange("e s p c -> p (e s) c").bitcast(I32))
         load_scales(w1_planes, w1_scales)
-        nc.scalar.copy(gate_first[:], gate_sb[:, 0:C])
+        for i in range(2):
+            nc.scalar.copy(gate_pair[i][:], gate_sb[:, 0:C])
 
         g_codes, g_scales = {}, {}
 
@@ -108,7 +111,7 @@ def tile_moe_bdx_mlp_relu_kernel(
                 g_codes[s, q] = codes[:, cols]
                 g_scales[s, q] = scales[:, cols]
 
-        dh, xts, das, codes2, staged, live = {}, {}, {}, {}, {}, {}
+        dh, xts, das, codes2, staged, live, dx = {}, {}, {}, {}, {}, {}, {}
 
         def multiply_w2(q, passes):
             e = q * P // C
@@ -120,61 +123,63 @@ def tile_moe_bdx_mlp_relu_kernel(
                         out=dh[q, h][:],
                         lhsT=g_codes[s, q].bitcast(E4M3),
                         lhsT_scale=g_scales[s, q],
-                        rhs=w2_sb[e][:, s, 1024 * h : 1024 * (h + 1)].bitcast(E2M1),
+                        rhs=w2_sb[e][s][:, 1024 * h : 1024 * (h + 1)].bitcast(E2M1),
                         rhs_scale=w2_planes[:, e * PASSES + s, 512 * h : 512 * (h + 1)],
                         start=(s == 0),
                         stop=(s == PASSES - 1),
                     )
 
         def turn(q):
-            xts[q] = banks.tile([P, HALVES, P, 2], F32, name="xt", tag="bank")
+            xts[q] = banks.tile([P, 2, HALVES, P], F32, name="xt", tag="bank")
             for h in range(HALVES):
-                if (q, h) not in ((0, 0), (1, 1)):
+                if (q, h) != (0, 0):
                     dhb = held.tile([P, 512], BF16, name=f"dhb{q}_{h}")[:]
                     staged[q, h] = dhb
                 else:
-                    dhb = wide_last[:, 0:512]
+                    dhb = wide_last[1][:]
                 nc.scalar.copy(
                     dhb.rearrange("c (u p b) -> c u p b", u=2, b=2),
                     dh[q, h][:].rearrange("c (p u b) -> c u p b", u=2, b=2),
                 )
                 for u in range(2):
-                    nc.tensor.transpose(xts[q][:, h, :, u], dhb[:, 256 * u : 256 * (u + 1)].bitcast(F32), identity[:])
+                    nc.tensor.transpose(xts[q][:, u, h, :], dhb[:, 256 * u : 256 * (u + 1)].bitcast(F32), identity[:])
 
-        def make_mask(e, tag):
-            live[e] = held.tile([P, HALVES, 4 * C], BF16, name=f"live{e}", tag=tag, align_bytes=64)
-            for h in range(HALVES):
+        def make_mask(e, tag, halves=range(HALVES)):
+            if e not in live:
+                live[e] = held.tile([P, 2, 2, HALVES * P * 2], BF16, name=f"live{e}", tag=tag, align_bytes=64)
+            for h in halves:
                 nc.vector.tensor_scalar(
-                    live[e][:, h, :].rearrange("p (c i d) -> p c d i", i=4, d=4),
-                    a_sb[e][h][:].rearrange("p d (c i) -> p c d i", i=4),
+                    live[e][:, :, :, 2 * P * h : 2 * P * (h + 1)],
+                    a_sb[e][h][:].rearrange("p (u b) c -> p u c b", b=2),
                     0.0,
                     None,
                     IS_GT,
                 )
 
-        def mask(q):
-            das[q] = held.tile([P, HALVES * 512], BF16, name=f"da{q}", align_bytes=64)
+        def mask(q, tag=None):
+            das[q] = held.tile([P, HALVES * 512], BF16, name=f"da{q}", tag=tag or f"da{q}", align_bytes=64)
             nc.vector.tensor_tensor(
-                das[q][:].rearrange("p (h x) -> p h x", h=HALVES),
-                xts[q][:].rearrange("p h c u -> p h (c u)").bitcast(BF16),
-                live[q // 2][:, :, 512 * (q % 2) : 512 * (q % 2 + 1)],
+                das[q][:].rearrange("p (x u b) -> p x u b", u=2, b=2),
+                xts[q][:].rearrange("p u h c -> p u (h c)").bitcast(BF16).rearrange("p u (x b) -> p x u b", b=2),
+                live[q // 2][:, :, q % 2, :].rearrange("p u (x b) -> p x u b", b=2),
                 MULT,
             )
 
-        def quantize_da(q):
-            codes = work.tile([P, HALVES * P], U32, name="da_codes", align_bytes=64)
-            scales = work.tile([P, HALVES * P], U8, name="da_scales", align_bytes=64)
+        def quantize_da(q, tag=None):
+            codes = held.tile([P, HALVES * P], U32, name=f"da_codes{q}", tag=tag or f"da_codes{q}", align_bytes=64)
+            scales = held.tile([P, HALVES * P], U8, name=f"da_scales{q}", align_bytes=64)
             nc.vector.quantize_mx(out=codes[:].bitcast(E4M3), scales=scales[:], in_=das[q][:])
             codes2[q] = codes, scales
 
-        def multiply_w1(q, dx_sb):
+        def multiply_w1(q):
             e = q * P // C
             codes, scales = codes2[q]
-            dx = banks.tile([P, P], F32, name="dx", tag="bank")
+            if q % 2 == 0:
+                dx[e] = banks.tile([P, C], F32, name="dx", tag="bank")
             for h in range(HALVES):
                 cols = slice(h * P, (h + 1) * P)
                 nc.tensor.matmul_mx(
-                    out=dx[:],
+                    out=dx[e][:, q % 2 * P : (q % 2 + 1) * P],
                     lhsT=w1_sb[:, e * HALVES + h, :].bitcast(E2M1),
                     lhsT_scale=w1_planes[:, e * HALVES + h, :],
                     rhs=codes[:, cols].bitcast(E4M3),
@@ -182,66 +187,67 @@ def tile_moe_bdx_mlp_relu_kernel(
                     start=(h == 0),
                     stop=(h == HALVES - 1),
                 )
-            nc.scalar.copy(dx_sb, dx[:])
 
-        def scatter(lo, n, dx_sb):
-            nc.vector.tensor_copy(window[:].indirect(offsets[:, lo // 16 : (lo + n) // 16]), dx_sb)
+        def scatter(e):
+            dx_sb = held.tile([P, C], F32, name=f"dx_sb{e}", tag=("live1", "dx_sb1")[e], align_bytes=64)
+            nc.scalar.copy(dx_sb[:], dx[e][:])
+            nc.vector.tensor_copy(window[:].indirect(offsets[:, e * C // 16 : (e + 1) * C // 16]), dx_sb[:])
 
-        dx012 = held.tile([P, 3 * P], F32, name="dx012")
-        dx3 = held.tile([P, P], F32, name="dx3")
-        g_all = [held.tile([P, 4 * S], F32, name=f"g_all{s}") for s in range(2)]
+        g_all = [held.tile([P, 4 * S], F32, name=f"g_all{s}", align_bytes=64) for s in range(2)]
         wide_zero = held.tile([P, 4 * S], BF16, name="wide_zero", align_bytes=64)
         g_first = held.tile([P, 4 * C], F32, name="g_first")
-        wide_last = held.tile([P, 4 * C], BF16, name="wide_last", align_bytes=64)
+        wide_last = [held.tile([P, 4 * P], BF16, name=f"wide_last{half}", align_bytes=64) for half in range(2)]
         wide_one = held.tile([P, 4 * C], BF16, name="wide_one", align_bytes=64)
-        g_last = held.tile([P, 4 * C], F32, name="g_last", align_bytes=64)
-        wide_mid = g_last[:, 0 : 2 * C].bitcast(BF16)
-        wide_first = g_last[:, 2 * C : 4 * C].bitcast(BF16)
+        wide_mid = held.tile([P, 4 * C], BF16, name="wide_mid", align_bytes=64)
 
         for lo in (0, C):
             gather_row(0, 0, lo, C, gate_sb[:, lo : lo + C], g_all[0][:, lo : lo + C])
         gather(0, 0, S, gate_sb[:], g_all[0][:], (1, 2, 3))
         interleave(wide_zero[:], g_all[0][:])
         gather(1, 0, S, gate_sb[:], g_all[1][:])
-        interleave(wide_mid, g_all[1][:], slice(0, C))
+        interleave(wide_mid[:], g_all[1][:], slice(0, C))
         interleave(wide_one[:], g_all[1][:], slice(C, S))
-        quantize_g(0, 0, C, wide_zero[:, 0 : 4 * C])
-        gather(2, 0, C, gate_first[:], g_first[:])
+        quantize_g(0, 0, S, wide_zero[:], "dy1_1")
+        gather(2, 0, C, gate_pair[0][:], g_first[:], (0, 1))
+        gather(2, 0, C, gate_pair[1][:], g_first[:], (2, 3))
+        quantize_g(1, 0, C, wide_mid[:], "gate_pair0")
+        g_last = held.tile([P, 8 * P], F32, name="g_last", tag="gate_pair1", align_bytes=64)
+        wide_first = g_last[:, 4 * P : 8 * P].bitcast(BF16)
         interleave(wide_first, g_first[:])
-        quantize_g(1, 0, C, wide_mid, "gate_first")
         quantize_g(2, 0, C, wide_first)
-        gather(2, C, C, gate_sb[:, C:S], g_last[:])
-        for s in range(PASSES):
+        gather(2, C, P, gate_sb[:, C : C + P], g_last[:, 0 : 4 * P])
+        interleave(wide_last[0][:], g_last[:, 0 : 4 * P])
+        gather(2, C + P, P, gate_sb[:, C + P : S], g_last[:, 4 * P : 8 * P], (0, 1))
+        quantize_g(1, C, C, wide_one[:], "dy2_0")
+        gather(2, C + P, P, gate_sb[:, C + P : S], g_last[:, 4 * P : 8 * P], (2, 3))
+        quantize_g(2, C, P, wide_last[0][:], "wide_one")
+        for q in range(GROUPS):
+            multiply_w2(q, (0,))
+        for s in (1, 2):
             multiply_w2(0, (s,))
             multiply_w2(1, (s,))
         turn(0)
-        interleave(wide_last[:], g_last[:])
-        quantize_g(0, C, C, wide_zero[:, 4 * C : 8 * C], "dy2_2")
-        multiply_w2(2, (0,))
-        multiply_w2(3, (0,))
-        make_mask(0, "dy2_3")
-        quantize_g(1, C, C, wide_one[:], "a_sb0_1")
+        interleave(wide_last[1][:], g_last[:, 4 * P : 8 * P])
         multiply_w2(2, (1,))
         multiply_w2(3, (1,))
-        mask(0)
-        quantize_g(2, C, C, wide_last[:], "wide_one")
         multiply_w2(2, (2,))
+        make_mask(0, "dy2_2")
+        mask(0)
+        quantize_g(2, C + P, P, wide_last[1][:], "a_sb0_1")
         multiply_w2(3, (2,))
         turn(1)
         turn(2)
         turn(3)
         quantize_da(0)
         mask(1)
-        quantize_da(1)
         make_mask(1, "live1")
-        multiply_w1(0, dx012[:, 0:P])
-        multiply_w1(1, dx012[:, P:C])
+        quantize_da(1, "a_sb1_1")
         mask(2)
-        quantize_da(2)
-        multiply_w1(2, dx012[:, C : 3 * P])
         mask(3)
+        quantize_da(2)
         quantize_da(3)
-        multiply_w1(3, dx3[:])
-        scatter(0, 3 * P, dx012[:])
-        scatter(C + P, P, dx3[:])
+        for q in range(GROUPS):
+            multiply_w1(q)
+            if q % 2 == 1:
+                scatter(q // 2)
         nc.sync.dma_start(out, window[:])

@@ -31,7 +31,7 @@ def tile_moe_bdx_mlp_relu_kernel(
     nc = tc.nc
     with ExitStack() as ctx:
         held = ctx.enter_context(tc.tile_pool(name="held", bufs=1))
-        banks = ctx.enter_context(tc.psum_pool(name="banks", bufs=8))
+        banks = ctx.enter_context(tc.psum_pool(name="banks", bufs=1))
 
         offsets = held.tile([P, S // 16], U16, name="offsets")
 
@@ -71,10 +71,10 @@ def tile_moe_bdx_mlp_relu_kernel(
             for r in range(4):
                 nc.sync.dma_start(planes[r:P:32, :, :].bitcast(I32), by_row[r].bitcast(I32))
 
-        load_dy(0, (0,))
-        nc.sync.dma_start(gate_sb[:, 0:C], gate[0:P, 0:C])
         nc.sync.dma_start(offsets[:], offs)
-        nc.sync.dma_start(gate_sb[:, C:S], gate[0:P, C:S])
+        load_dy(0, (0,))
+        nc.sync.dma_start(gate_sb[:, 0:P], gate[0:P, 0:P])
+        nc.sync.dma_start(gate_sb[:, P:S], gate[0:P, P:S])
         load_dy(0, (1, 2, 3))
         load_dy(1)
         load_scales(w2_planes, w2_scales)
@@ -117,7 +117,7 @@ def tile_moe_bdx_mlp_relu_kernel(
             e = q * P // C
             for h in range(HALVES):
                 if 0 in passes:
-                    dh[q, h] = banks.tile([P, 512], F32, name="dh", tag="bank")
+                    dh[q, h] = banks.tile([P, 512], F32, name="dh", tag=f"bank{q}_{h}")
                 for s in passes:
                     nc.tensor.matmul_mx(
                         out=dh[q, h][:],
@@ -130,10 +130,10 @@ def tile_moe_bdx_mlp_relu_kernel(
                     )
 
         def turn(q):
-            xts[q] = banks.tile([P, 2, HALVES, P], F32, name="xt", tag="bank")
+            xts[q] = banks.tile([P, 2, HALVES, P], F32, name="xt", tag=f"bank{q}_0")
             for h in range(HALVES):
                 if (q, h) != (0, 0):
-                    dhb = held.tile([P, 512], BF16, name=f"dhb{q}_{h}")[:]
+                    dhb = held.tile([P, 512], BF16, name=f"dhb{q}_{h}", align_bytes=64)[:]
                     staged[q, h] = dhb
                 else:
                     dhb = wide_last[1][:]
@@ -175,7 +175,7 @@ def tile_moe_bdx_mlp_relu_kernel(
             e = q * P // C
             codes, scales = codes2[q]
             if q % 2 == 0:
-                dx[e] = banks.tile([P, C], F32, name="dx", tag="bank")
+                dx[e] = banks.tile([P, C], F32, name="dx", tag=("bank3_1", "bank2_1")[e])
             for h in range(HALVES):
                 cols = slice(h * P, (h + 1) * P)
                 nc.tensor.matmul_mx(
@@ -189,7 +189,7 @@ def tile_moe_bdx_mlp_relu_kernel(
                 )
 
         def scatter(e):
-            dx_sb = held.tile([P, C], F32, name=f"dx_sb{e}", tag=("live1", "dx_sb1")[e], align_bytes=64)
+            dx_sb = held.tile([P, C], F32, name=f"dx_sb{e}", align_bytes=64)
             nc.scalar.copy(dx_sb[:], dx[e][:])
             nc.vector.tensor_copy(window[:].indirect(offsets[:, e * C // 16 : (e + 1) * C // 16]), dx_sb[:])
 
@@ -200,8 +200,8 @@ def tile_moe_bdx_mlp_relu_kernel(
         wide_one = held.tile([P, 4 * C], BF16, name="wide_one", align_bytes=64)
         wide_mid = held.tile([P, 4 * C], BF16, name="wide_mid", align_bytes=64)
 
-        for lo in (0, C):
-            gather_row(0, 0, lo, C, gate_sb[:, lo : lo + C], g_all[0][:, lo : lo + C])
+        for lo, hi in ((0, P), (P, S)):
+            gather_row(0, 0, lo, hi - lo, gate_sb[:, lo:hi], g_all[0][:, lo:hi])
         gather(0, 0, S, gate_sb[:], g_all[0][:], (1, 2, 3))
         interleave(wide_zero[:], g_all[0][:])
         gather(1, 0, S, gate_sb[:], g_all[1][:])
@@ -241,10 +241,10 @@ def tile_moe_bdx_mlp_relu_kernel(
         quantize_da(0)
         mask(1)
         make_mask(1, "live1")
-        quantize_da(1, "a_sb1_1")
+        quantize_da(1, "a_sb1_0")
         mask(2)
         mask(3)
-        quantize_da(2)
+        quantize_da(2, "dhb3_1")
         quantize_da(3)
         for q in range(GROUPS):
             multiply_w1(q)

@@ -36,7 +36,8 @@ def tile_moe_bdx_mlp_relu_kernel(
         offsets = held.tile([P, S // 16], U16, name="offsets")
 
         gate_sb = held.tile([P, S], F32, name="gate_sb")
-        gate_pair = [held.tile([P, C], F32, name=f"gate_pair{i}", align_bytes=64) for i in range(2)]
+        gate_first = held.tile([P, C], F32, name="gate_first", align_bytes=64)
+        gate_late = held.tile([P, C], F32, name="gate_late", align_bytes=64)
         w2_planes = held.tile([P, E * PASSES, H], U8, name="w2_planes", align_bytes=64)
         w1_planes = held.tile([P, E * HALVES, K], U8, name="w1_planes", align_bytes=64)
         window = held.tile([P, T], F32, name="window")
@@ -52,8 +53,10 @@ def tile_moe_bdx_mlp_relu_kernel(
         w2_rest = [held.tile([P, PASSES - 1, 2 * H], U8, name=f"w2_rest{e}", align_bytes=64) for e in range(E)]
         w2_sb = [[w2_zero[:, e, :], w2_rest[e][:, 0, :], w2_rest[e][:, 1, :]] for e in range(E)]
         w1_sb = held.tile([P, E * HALVES, 2 * K], U8, name="w1_sb", align_bytes=64)
-        a_sb = [[held.tile([P, 4, C], F32, name=f"a_sb{e}_{h}", align_bytes=64) for h in range(HALVES)] for e in range(E)]
-        a_view = a.rearrange("(h p d) (e c) -> e h p d c", p=P, d=4, e=E)
+        a_low = held.tile([P, 4, S], F32, name="a_low", align_bytes=64)
+        a_high = [held.tile([P, 4, C], F32, name=f"a_high{e}", align_bytes=64) for e in range(E)]
+        a_sb = [[a_low[:, :, e * C : (e + 1) * C], a_high[e][:]] for e in range(E)]
+        a_view = a.rearrange("(h p d) c -> h p d c", p=P, d=4)
 
         def load_dy(s, rows=range(4)):
             for d in rows:
@@ -61,10 +64,6 @@ def tile_moe_bdx_mlp_relu_kernel(
 
         def load_w2(e):
             nc.sync.dma_start(w2_rest[e][:].bitcast(I32), w2_words[e, 1:].rearrange("s p c -> p s c").bitcast(I32))
-
-        def load_a(e):
-            for h in range(HALVES):
-                nc.sync.dma_start(a_sb[e][h][:], a_view[e, h])
 
         def load_scales(planes, scales):
             by_row = scales.rearrange("e s (quad r) c -> r quad (e s) c", r=4)
@@ -78,16 +77,18 @@ def tile_moe_bdx_mlp_relu_kernel(
         load_dy(0, (1, 2, 3))
         load_dy(1)
         load_scales(w2_planes, w2_scales)
-        load_dy(2)
+        load_dy(2, (0, 1))
         nc.sync.dma_start(w2_zero[:].bitcast(I32), w2_words[:, 0].rearrange("e p c -> p e c").bitcast(I32))
+        load_dy(2, (2, 3))
+        nc.sync.dma_start(gate_late[:], gate[P : 2 * P, C:S])
+        load_w2(0)
+        load_w2(1)
+        nc.sync.dma_start(a_low[:], a_view[0])
         for e in range(E):
-            load_w2(e)
-        load_a(0)
-        load_a(1)
+            nc.sync.dma_start(a_high[e][:], a_view[1][:, :, e * C : (e + 1) * C])
         nc.sync.dma_start(w1_sb[:].bitcast(I32), w1_words.rearrange("e s p c -> p (e s) c").bitcast(I32))
         load_scales(w1_planes, w1_scales)
-        for i in range(2):
-            nc.scalar.copy(gate_pair[i][:], gate_sb[:, 0:C])
+        nc.scalar.copy(gate_first[:], gate_sb[:, 0:C])
 
         g_codes, g_scales = {}, {}
 
@@ -113,12 +114,12 @@ def tile_moe_bdx_mlp_relu_kernel(
 
         dh, xts, das, codes2, staged, live, dx = {}, {}, {}, {}, {}, {}, {}
 
-        def multiply_w2(q, passes):
-            e = q * P // C
-            for h in range(HALVES):
-                if 0 in passes:
-                    dh[q, h] = banks.tile([P, 512], F32, name="dh", tag=f"bank{q}_{h}")
-                for s in passes:
+        def multiply_w2(s, groups, halves=range(HALVES)):
+            for h in halves:
+                for q in groups:
+                    e = q * P // C
+                    if s == 0:
+                        dh[q, h] = banks.tile([P, 512], F32, name="dh", tag=f"bank{q}_{h}")
                     nc.tensor.matmul_mx(
                         out=dh[q, h][:],
                         lhsT=g_codes[s, q].bitcast(E4M3),
@@ -129,64 +130,61 @@ def tile_moe_bdx_mlp_relu_kernel(
                         stop=(s == PASSES - 1),
                     )
 
-        def turn(q):
-            xts[q] = banks.tile([P, 2, HALVES, P], F32, name="xt", tag=f"bank{q}_0")
-            for h in range(HALVES):
-                if (q, h) != (0, 0):
-                    dhb = held.tile([P, 512], BF16, name=f"dhb{q}_{h}", align_bytes=64)[:]
-                    staged[q, h] = dhb
-                else:
-                    dhb = wide_last[1][:]
-                nc.scalar.copy(
-                    dhb.rearrange("c (u p b) -> c u p b", u=2, b=2),
-                    dh[q, h][:].rearrange("c (p u b) -> c u p b", u=2, b=2),
-                )
-                for u in range(2):
-                    nc.tensor.transpose(xts[q][:, u, h, :], dhb[:, 256 * u : 256 * (u + 1)].bitcast(F32), identity[:])
-
-        def make_mask(e, tag, halves=range(HALVES)):
-            if e not in live:
-                live[e] = held.tile([P, 2, 2, HALVES * P * 2], BF16, name=f"live{e}", tag=tag, align_bytes=64)
-            for h in halves:
-                nc.vector.tensor_scalar(
-                    live[e][:, :, :, 2 * P * h : 2 * P * (h + 1)],
-                    a_sb[e][h][:].rearrange("p (u b) c -> p u c b", b=2),
-                    0.0,
-                    None,
-                    IS_GT,
+        def turn(q, h):
+            e = q * P // C
+            if q % 2 == 0:
+                xts[e, h] = banks.tile([P, 2, C], F32, name="xt", tag=f"bank{q}_{h}")
+            if (q, h) != (0, 0):
+                dhb = held.tile([P, 512], BF16, name=f"dhb{q}_{h}", align_bytes=64)[:]
+            else:
+                dhb = wide_last[1][:]
+            staged[q, h] = dhb
+            nc.scalar.copy(
+                dhb.rearrange("c (u p b) -> c u p b", u=2, b=2),
+                dh[q, h][:].rearrange("c (p u b) -> c u p b", u=2, b=2),
+            )
+            for u in range(2):
+                nc.tensor.transpose(
+                    xts[e, h][:, u, q % 2 * P : (q % 2 + 1) * P], dhb[:, 256 * u : 256 * (u + 1)].bitcast(F32), identity[:]
                 )
 
-        def mask(q, tag=None):
-            das[q] = held.tile([P, HALVES * 512], BF16, name=f"da{q}", tag=tag or f"da{q}", align_bytes=64)
+        def make_mask(e, h, tag=None):
+            live[e, h] = held.tile([P, 2, C, 2], BF16, name=f"live{e}_{h}", tag=tag or f"live{e}_{h}", align_bytes=64)
+            rows = a_sb[e][h]
+            nc.vector.tensor_scalar(live[e, h][:], rows.rearrange("p (u b) c -> p u c b", b=2), 0.0, None, IS_GT)
+
+        def mask(e, h, da):
+            das[e, h] = da
             nc.vector.tensor_tensor(
-                das[q][:].rearrange("p (x u b) -> p x u b", u=2, b=2),
-                xts[q][:].rearrange("p u h c -> p u (h c)").bitcast(BF16).rearrange("p u (x b) -> p x u b", b=2),
-                live[q // 2][:, :, q % 2, :].rearrange("p u (x b) -> p x u b", b=2),
+                da.rearrange("p (x u b) -> p x u b", u=2, b=2),
+                xts[e, h][:].rearrange("p u c -> p (u c)").bitcast(BF16).rearrange("p (u x b) -> p x u b", u=2, b=2),
+                live[e, h][:].rearrange("p u x b -> p x u b"),
                 MULT,
             )
 
-        def quantize_da(q, tag=None):
-            codes = held.tile([P, HALVES * P], U32, name=f"da_codes{q}", tag=tag or f"da_codes{q}", align_bytes=64)
-            scales = held.tile([P, HALVES * P], U8, name=f"da_scales{q}", align_bytes=64)
-            nc.vector.quantize_mx(out=codes[:].bitcast(E4M3), scales=scales[:], in_=das[q][:])
-            codes2[q] = codes, scales
+        def quantize_da(e, halves, da, tag=None):
+            n = len(halves) * C
+            codes = held.tile([P, n], U32, name=f"da_codes{e}_{halves[0]}", tag=tag or f"da_codes{e}_{halves[0]}", align_bytes=64)
+            scales = held.tile([P, n], U8, name=f"da_scales{e}_{halves[0]}", align_bytes=64)
+            nc.vector.quantize_mx(out=codes[:].bitcast(E4M3), scales=scales[:], in_=da)
+            for i, h in enumerate(halves):
+                codes2[e, h] = codes[:, i * C : (i + 1) * C], scales[:, i * C : (i + 1) * C]
 
-        def multiply_w1(q):
-            e = q * P // C
-            codes, scales = codes2[q]
-            if q % 2 == 0:
-                dx[e] = banks.tile([P, C], F32, name="dx", tag=("bank3_1", "bank2_1")[e])
-            for h in range(HALVES):
-                cols = slice(h * P, (h + 1) * P)
-                nc.tensor.matmul_mx(
-                    out=dx[e][:, q % 2 * P : (q % 2 + 1) * P],
-                    lhsT=w1_sb[:, e * HALVES + h, :].bitcast(E2M1),
-                    lhsT_scale=w1_planes[:, e * HALVES + h, :],
-                    rhs=codes[:, cols].bitcast(E4M3),
-                    rhs_scale=scales[:, cols],
-                    start=(h == 0),
-                    stop=(h == HALVES - 1),
-                )
+        def multiply_w1(e):
+            dx[e] = banks.tile([P, C], F32, name="dx", tag=("bank3_1", "bank3_0")[e])
+            for half in range(2):
+                cols = slice(half * P, (half + 1) * P)
+                for h in range(HALVES):
+                    codes, scales = codes2[e, h]
+                    nc.tensor.matmul_mx(
+                        out=dx[e][:, cols],
+                        lhsT=w1_sb[:, e * HALVES + h, :].bitcast(E2M1),
+                        lhsT_scale=w1_planes[:, e * HALVES + h, :],
+                        rhs=codes[:, cols].bitcast(E4M3),
+                        rhs_scale=scales[:, cols],
+                        start=(h == 0),
+                        stop=(h == HALVES - 1),
+                    )
 
         def scatter(e):
             dx_sb = held.tile([P, C], F32, name=f"dx_sb{e}", align_bytes=64)
@@ -195,7 +193,11 @@ def tile_moe_bdx_mlp_relu_kernel(
 
         g_all = [held.tile([P, 4 * S], F32, name=f"g_all{s}", align_bytes=64) for s in range(2)]
         wide_zero = held.tile([P, 4 * S], BF16, name="wide_zero", align_bytes=64)
-        g_first = held.tile([P, 4 * C], F32, name="g_first")
+        g_rest = held.tile([P, P + 4 * C], F32, name="g_rest", align_bytes=64)
+        g_first = g_rest[:, P:]
+        g_last = g_rest[:, 0 : 4 * P]
+        g_third = held.tile([P, 4 * P], F32, name="g_third", align_bytes=64)
+        wide_first = held.tile([P, 4 * C], BF16, name="wide_first", align_bytes=64)
         wide_last = [held.tile([P, 4 * P], BF16, name=f"wide_last{half}", align_bytes=64) for half in range(2)]
         wide_one = held.tile([P, 4 * C], BF16, name="wide_one", align_bytes=64)
         wide_mid = held.tile([P, 4 * C], BF16, name="wide_mid", align_bytes=64)
@@ -208,46 +210,48 @@ def tile_moe_bdx_mlp_relu_kernel(
         interleave(wide_mid[:], g_all[1][:], slice(0, C))
         interleave(wide_one[:], g_all[1][:], slice(C, S))
         quantize_g(0, 0, S, wide_zero[:], "dy1_1")
-        gather(2, 0, C, gate_pair[0][:], g_first[:], (0, 1))
-        gather(2, 0, C, gate_pair[1][:], g_first[:], (2, 3))
-        quantize_g(1, 0, C, wide_mid[:], "gate_pair0")
-        g_last = held.tile([P, 8 * P], F32, name="g_last", tag="gate_pair1", align_bytes=64)
-        wide_first = g_last[:, 4 * P : 8 * P].bitcast(BF16)
-        interleave(wide_first, g_first[:])
-        quantize_g(2, 0, C, wide_first)
-        gather(2, C, P, gate_sb[:, C : C + P], g_last[:, 0 : 4 * P])
-        interleave(wide_last[0][:], g_last[:, 0 : 4 * P])
-        gather(2, C + P, P, gate_sb[:, C + P : S], g_last[:, 4 * P : 8 * P], (0, 1))
-        quantize_g(1, C, C, wide_one[:], "dy2_0")
-        gather(2, C + P, P, gate_sb[:, C + P : S], g_last[:, 4 * P : 8 * P], (2, 3))
+        gather(2, 0, C, gate_first[:], g_first, (0, 1, 2))
+        quantize_g(1, 0, C, wide_mid[:], "gate_first")
+        gather(2, 0, C, gate_sb[:, 0:C], g_first, (3,))
+        interleave(wide_first[:], g_first)
+        gather(2, C, P, gate_late[:, 0:P], g_third[:])
+        interleave(wide_last[0][:], g_third[:])
+        gather(2, C + P, P, gate_late[:, P:C], g_last, (0,))
+        quantize_g(2, 0, C, wide_first[:])
+        gather(2, C + P, P, gate_late[:, P:C], g_last, (1, 2))
+        quantize_g(1, C, C, wide_one[:], "dy2_1")
+        gather(2, C + P, P, gate_late[:, P:C], g_last, (3,))
         quantize_g(2, C, P, wide_last[0][:], "wide_one")
-        for q in range(GROUPS):
-            multiply_w2(q, (0,))
-        for s in (1, 2):
-            multiply_w2(0, (s,))
-            multiply_w2(1, (s,))
-        turn(0)
-        interleave(wide_last[1][:], g_last[:, 4 * P : 8 * P])
-        multiply_w2(2, (1,))
-        multiply_w2(3, (1,))
+        multiply_w2(0, (0, 1))
+        multiply_w2(0, (2, 3))
+        multiply_w2(1, (0, 1))
+        multiply_w2(2, (0, 1))
+        turn(0, 0)
+        turn(1, 0)
+        interleave(wide_last[1][:], g_last)
+        multiply_w2(1, (2, 3))
         multiply_w2(2, (2,))
-        make_mask(0, "dy2_2")
-        mask(0)
-        quantize_g(2, C + P, P, wide_last[1][:], "a_sb0_1")
-        multiply_w2(3, (2,))
-        turn(1)
-        turn(2)
-        turn(3)
-        quantize_da(0)
-        mask(1)
-        make_mask(1, "live1")
-        quantize_da(1, "a_sb1_0")
-        mask(2)
-        mask(3)
-        quantize_da(2, "dhb3_1")
-        quantize_da(3)
-        for q in range(GROUPS):
-            multiply_w1(q)
-            if q % 2 == 1:
-                scatter(q // 2)
+        make_mask(0, 0, "dy2_2")
+        make_mask(1, 0, "dy2_3")
+        quantize_g(2, C + P, P, wide_last[1][:])
+        multiply_w2(2, (3,))
+        turn(0, 1)
+        turn(1, 1)
+        mask(0, 0, g_last.bitcast(BF16))
+        make_mask(0, 1)
+        quantize_da(0, (0,), das[0, 0])
+        mask(0, 1, held.tile([P, 4 * C], BF16, name="da01", align_bytes=64)[:])
+        turn(2, 0)
+        turn(3, 0)
+        turn(2, 1)
+        turn(3, 1)
+        make_mask(1, 1)
+        quantize_da(0, (1,), das[0, 1])
+        mask(1, 0, held.tile([P, 4 * C], BF16, name="da10", tag="a_high0", align_bytes=64)[:])
+        mask(1, 1, held.tile([P, 4 * C], BF16, name="da11", align_bytes=64)[:])
+        quantize_da(1, (0,), das[1, 0], "dhb3_1")
+        quantize_da(1, (1,), das[1, 1])
+        for e in range(E):
+            multiply_w1(e)
+            scatter(e)
         nc.sync.dma_start(out, window[:])

@@ -20,9 +20,12 @@ MULT = mybir.AluOpType.mult
 IS_GT = mybir.AluOpType.is_gt
 
 P = 128
-PASSES = N // 512
-HALVES = H // 512
-GROUPS = S // P
+PACK = 4
+SPAN = P * PACK
+PASSES = N // SPAN
+HALVES = H // SPAN
+LIST_ROWS = 16
+MX_ALIGN = 64
 
 
 def tile_moe_bdx_mlp_relu_kernel(
@@ -33,13 +36,16 @@ def tile_moe_bdx_mlp_relu_kernel(
         held = ctx.enter_context(tc.tile_pool(name="held", bufs=1))
         banks = ctx.enter_context(tc.psum_pool(name="banks", bufs=1))
 
-        offsets = held.tile([P, S // 16], U16, name="offsets")
+        def sbuf(shape, dtype, name, tag=None):
+            return held.tile(shape, dtype, name=name, tag=tag or name, align_bytes=MX_ALIGN)
+
+        offsets = held.tile([P, S // LIST_ROWS], U16, name="offsets")
 
         gate_sb = held.tile([P, S], F32, name="gate_sb")
-        gate_first = held.tile([P, C], F32, name="gate_first", align_bytes=64)
-        gate_late = held.tile([P, C], F32, name="gate_late", align_bytes=64)
-        w2_planes = held.tile([P, E * PASSES, H], U8, name="w2_planes", align_bytes=64)
-        w1_planes = held.tile([P, E * HALVES, K], U8, name="w1_planes", align_bytes=64)
+        gate_first = sbuf([P, C], F32, "gate_first")
+        gate_late = sbuf([P, P], F32, "gate_late")
+        w2_planes = sbuf([P, E * PASSES, H], U8, "w2_planes")
+        w1_planes = sbuf([P, E * HALVES, K], U8, "w1_planes")
         window = held.tile([P, T], F32, name="window")
         identity = held.tile([P, P], F32, name="identity")
         nc.vector.memset(w2_planes[:].rearrange("p n c -> p (n c)").bitcast(I32), 0)
@@ -47,23 +53,20 @@ def tile_moe_bdx_mlp_relu_kernel(
         nc.vector.memset(window[:], 0.0)
         make_identity(nc, identity[:])
 
-        dy_view = dyT.rearrange("(s p d) t -> s d p t", p=P, d=4)
-        dy = [[held.tile([P, T], F32, name=f"dy{s}_{d}", align_bytes=64) for d in range(4)] for s in range(PASSES)]
-        w2_zero = held.tile([P, E, 2 * H], U8, name="w2_zero", align_bytes=64)
-        w2_rest = [held.tile([P, PASSES - 1, 2 * H], U8, name=f"w2_rest{e}", align_bytes=64) for e in range(E)]
+        dy_view = dyT.rearrange("(s p d) t -> s d p t", p=P, d=PACK)
+        dy = [[sbuf([P, T], F32, f"dy{s}_{d}") for d in range(PACK)] for s in range(PASSES)]
+        w2_zero = sbuf([P, E, 2 * H], U8, "w2_zero")
+        w2_rest = [sbuf([P, PASSES - 1, 2 * H], U8, f"w2_rest{e}") for e in range(E)]
         w2_sb = [[w2_zero[:, e, :], w2_rest[e][:, 0, :], w2_rest[e][:, 1, :]] for e in range(E)]
-        w1_sb = held.tile([P, E * HALVES, 2 * K], U8, name="w1_sb", align_bytes=64)
-        a_low = held.tile([P, 4, S], F32, name="a_low", align_bytes=64)
-        a_high = [held.tile([P, 4, C], F32, name=f"a_high{e}", align_bytes=64) for e in range(E)]
+        w1_sb = sbuf([P, E * HALVES, 2 * K], U8, "w1_sb")
+        a_low = sbuf([P, PACK, S], F32, "a_low")
+        a_high = [sbuf([P, PACK, C], F32, f"a_high{e}") for e in range(E)]
         a_sb = [[a_low[:, :, e * C : (e + 1) * C], a_high[e][:]] for e in range(E)]
-        a_view = a.rearrange("(h p d) c -> h p d c", p=P, d=4)
+        a_view = a.rearrange("(h p d) c -> h p d c", p=P, d=PACK)
 
-        def load_dy(s, rows=range(4)):
+        def load_dy(s, rows=range(PACK)):
             for d in rows:
                 nc.sync.dma_start(dy[s][d][:], dy_view[s, d])
-
-        def load_w2(e):
-            nc.sync.dma_start(w2_rest[e][:].bitcast(I32), w2_words[e, 1:].rearrange("s p c -> p s c").bitcast(I32))
 
         def load_scales(planes, scales):
             by_row = scales.rearrange("e s (quad r) c -> r quad (e s) c", r=4)
@@ -80,9 +83,9 @@ def tile_moe_bdx_mlp_relu_kernel(
         load_dy(2, (0, 1))
         nc.sync.dma_start(w2_zero[:].bitcast(I32), w2_words[:, 0].rearrange("e p c -> p e c").bitcast(I32))
         load_dy(2, (2, 3))
-        nc.sync.dma_start(gate_late[:], gate[P : 2 * P, C:S])
-        load_w2(0)
-        load_w2(1)
+        nc.sync.dma_start(gate_late[:], gate[P : 2 * P, C : C + P])
+        for e in range(E):
+            nc.sync.dma_start(w2_rest[e][:].bitcast(I32), w2_words[e, 1:].rearrange("s p c -> p s c").bitcast(I32))
         nc.sync.dma_start(a_low[:], a_view[0])
         for e in range(E):
             nc.sync.dma_start(a_high[e][:], a_view[1][:, :, e * C : (e + 1) * C])
@@ -90,168 +93,161 @@ def tile_moe_bdx_mlp_relu_kernel(
         load_scales(w1_planes, w1_scales)
         nc.scalar.copy(gate_first[:], gate_sb[:, 0:C])
 
-        g_codes, g_scales = {}, {}
+        g_codes, g_scales, dh, turned, live, da, da_codes, da_scales, dx = {}, {}, {}, {}, {}, {}, {}, {}, {}
 
         def gather_row(s, d, lo, n, gates, g_row):
-            nc.vector.tensor_tensor(g_row, dy[s][d][:].indirect(offsets[:, lo // 16 : (lo + n) // 16]), gates, MULT)
+            picked = dy[s][d][:].indirect(offsets[:, lo // LIST_ROWS : (lo + n) // LIST_ROWS])
+            nc.vector.tensor_tensor(g_row, picked, gates, MULT)
 
-        def gather(s, lo, n, gates, g, rows=range(4)):
+        def gather(s, lo, n, gates, g, rows=range(PACK)):
             for d in rows:
                 gather_row(s, d, lo, n, gates, g[:, d * n : (d + 1) * n])
 
         def interleave(wide, g, cols=slice(None)):
-            rows = g.rearrange("p (d c) -> p d c", d=4)[:, :, cols]
-            nc.scalar.copy(wide.rearrange("p (c i d) -> p c d i", i=4, d=4), rows.rearrange("p d (c i) -> p c d i", i=4))
+            rows = g.rearrange("p (d c) -> p d c", d=PACK)[:, :, cols]
+            nc.scalar.copy(
+                wide.rearrange("p (c i d) -> p c d i", i=4, d=PACK), rows.rearrange("p d (c i) -> p c d i", i=4)
+            )
 
         def quantize_g(s, lo, n, wide, tag=None):
-            codes = held.tile([P, n], U32, name=f"g_codes{s}_{lo}", tag=tag or f"g_codes{s}_{lo}", align_bytes=64)
-            scales = held.tile([P, n], U8, name=f"g_scales{s}_{lo}", align_bytes=64)
+            codes = sbuf([P, n], U32, f"g_codes{s}_{lo}", tag)
+            scales = sbuf([P, n], U8, f"g_scales{s}_{lo}")
             nc.vector.quantize_mx(out=codes[:].bitcast(E4M3), scales=scales[:], in_=wide)
             for q in range(lo // P, (lo + n) // P):
                 cols = slice(q * P - lo, q * P - lo + P)
                 g_codes[s, q] = codes[:, cols]
                 g_scales[s, q] = scales[:, cols]
 
-        dh, xts, das, codes2, staged, live, dx = {}, {}, {}, {}, {}, {}, {}
-
-        def multiply_w2(s, groups, halves=range(HALVES)):
-            for h in halves:
+        def multiply_w2(s, groups):
+            for h in range(HALVES):
                 for q in groups:
                     e = q * P // C
                     if s == 0:
-                        dh[q, h] = banks.tile([P, 512], F32, name="dh", tag=f"bank{q}_{h}")
+                        dh[q, h] = banks.tile([P, SPAN], F32, name="dh", tag=f"bank{q}_{h}")
                     nc.tensor.matmul_mx(
                         out=dh[q, h][:],
                         lhsT=g_codes[s, q].bitcast(E4M3),
                         lhsT_scale=g_scales[s, q],
-                        rhs=w2_sb[e][s][:, 1024 * h : 1024 * (h + 1)].bitcast(E2M1),
-                        rhs_scale=w2_planes[:, e * PASSES + s, 512 * h : 512 * (h + 1)],
+                        rhs=w2_sb[e][s][:, 2 * SPAN * h : 2 * SPAN * (h + 1)].bitcast(E2M1),
+                        rhs_scale=w2_planes[:, e * PASSES + s, SPAN * h : SPAN * (h + 1)],
                         start=(s == 0),
                         stop=(s == PASSES - 1),
                     )
 
-        def turn(q, h):
+        def turn(q, h, rounded=None):
             e = q * P // C
             if q % 2 == 0:
-                xts[e, h] = banks.tile([P, 2, C], F32, name="xt", tag=f"bank{q}_{h}")
-            if (q, h) != (0, 0):
-                dhb = held.tile([P, 512], BF16, name=f"dhb{q}_{h}", align_bytes=64)[:]
-            else:
-                dhb = wide_last[1][:]
-            staged[q, h] = dhb
+                turned[e, h] = banks.tile([P, 2, C], F32, name="turned", tag=f"bank{q}_{h}")
+            if rounded is None:
+                rounded = sbuf([P, SPAN], BF16, f"rounded{q}_{h}")[:]
             nc.scalar.copy(
-                dhb.rearrange("c (u p b) -> c u p b", u=2, b=2),
+                rounded.rearrange("c (u p b) -> c u p b", u=2, b=2),
                 dh[q, h][:].rearrange("c (p u b) -> c u p b", u=2, b=2),
             )
             for u in range(2):
-                nc.tensor.transpose(
-                    xts[e, h][:, u, q % 2 * P : (q % 2 + 1) * P], dhb[:, 256 * u : 256 * (u + 1)].bitcast(F32), identity[:]
-                )
+                words = rounded[:, 2 * P * u : 2 * P * (u + 1)].bitcast(F32)
+                nc.tensor.transpose(turned[e, h][:, u, q % 2 * P : (q % 2 + 1) * P], words, identity[:])
 
         def make_mask(e, h, tag=None):
-            live[e, h] = held.tile([P, 2, C, 2], BF16, name=f"live{e}_{h}", tag=tag or f"live{e}_{h}", align_bytes=64)
-            rows = a_sb[e][h]
-            nc.vector.tensor_scalar(live[e, h][:], rows.rearrange("p (u b) c -> p u c b", b=2), 0.0, None, IS_GT)
+            live[e, h] = sbuf([P, 2, C, 2], BF16, f"live{e}_{h}", tag)
+            nc.vector.tensor_scalar(live[e, h][:], a_sb[e][h].rearrange("p (u b) c -> p u c b", b=2), 0.0, None, IS_GT)
 
-        def mask(e, h, da):
-            das[e, h] = da
+        def apply_mask(e, h, product):
+            da[e, h] = product
             nc.vector.tensor_tensor(
-                da.rearrange("p (x u b) -> p x u b", u=2, b=2),
-                xts[e, h][:].rearrange("p u c -> p (u c)").bitcast(BF16).rearrange("p (u x b) -> p x u b", u=2, b=2),
-                live[e, h][:].rearrange("p u x b -> p x u b"),
+                product.rearrange("p (c u b) -> p c u b", u=2, b=2),
+                turned[e, h][:].rearrange("p u c -> p (u c)").bitcast(BF16).rearrange("p (u c b) -> p c u b", u=2, b=2),
+                live[e, h][:].rearrange("p u c b -> p c u b"),
                 MULT,
             )
 
-        def quantize_da(e, halves, da, tag=None):
-            n = len(halves) * C
-            codes = held.tile([P, n], U32, name=f"da_codes{e}_{halves[0]}", tag=tag or f"da_codes{e}_{halves[0]}", align_bytes=64)
-            scales = held.tile([P, n], U8, name=f"da_scales{e}_{halves[0]}", align_bytes=64)
-            nc.vector.quantize_mx(out=codes[:].bitcast(E4M3), scales=scales[:], in_=da)
-            for i, h in enumerate(halves):
-                codes2[e, h] = codes[:, i * C : (i + 1) * C], scales[:, i * C : (i + 1) * C]
+        def quantize_da(e, h, tag=None):
+            da_codes[e, h] = sbuf([P, C], U32, f"da_codes{e}_{h}", tag)
+            da_scales[e, h] = sbuf([P, C], U8, f"da_scales{e}_{h}")
+            nc.vector.quantize_mx(out=da_codes[e, h][:].bitcast(E4M3), scales=da_scales[e, h][:], in_=da[e, h])
 
-        def multiply_w1(e):
-            dx[e] = banks.tile([P, C], F32, name="dx", tag=("bank3_1", "bank3_0")[e])
-            for half in range(2):
-                cols = slice(half * P, (half + 1) * P)
+        def multiply_w1(e, bank):
+            dx[e] = banks.tile([P, C], F32, name="dx", tag=bank)
+            for cols in (slice(0, P), slice(P, C)):
                 for h in range(HALVES):
-                    codes, scales = codes2[e, h]
                     nc.tensor.matmul_mx(
                         out=dx[e][:, cols],
                         lhsT=w1_sb[:, e * HALVES + h, :].bitcast(E2M1),
                         lhsT_scale=w1_planes[:, e * HALVES + h, :],
-                        rhs=codes[:, cols].bitcast(E4M3),
-                        rhs_scale=scales[:, cols],
+                        rhs=da_codes[e, h][:, cols].bitcast(E4M3),
+                        rhs_scale=da_scales[e, h][:, cols],
                         start=(h == 0),
                         stop=(h == HALVES - 1),
                     )
 
         def scatter(e):
-            dx_sb = held.tile([P, C], F32, name=f"dx_sb{e}", align_bytes=64)
+            dx_sb = sbuf([P, C], F32, f"dx_sb{e}")
             nc.scalar.copy(dx_sb[:], dx[e][:])
-            nc.vector.tensor_copy(window[:].indirect(offsets[:, e * C // 16 : (e + 1) * C // 16]), dx_sb[:])
+            places = window[:].indirect(offsets[:, e * C // LIST_ROWS : (e + 1) * C // LIST_ROWS])
+            nc.vector.tensor_copy(places, dx_sb[:])
 
-        g_all = [held.tile([P, 4 * S], F32, name=f"g_all{s}", align_bytes=64) for s in range(2)]
-        wide_zero = held.tile([P, 4 * S], BF16, name="wide_zero", align_bytes=64)
-        g_rest = held.tile([P, P + 4 * C], F32, name="g_rest", align_bytes=64)
-        g_first = g_rest[:, P:]
-        g_last = g_rest[:, 0 : 4 * P]
-        g_third = held.tile([P, 4 * P], F32, name="g_third", align_bytes=64)
-        wide_first = held.tile([P, 4 * C], BF16, name="wide_first", align_bytes=64)
-        wide_last = [held.tile([P, 4 * P], BF16, name=f"wide_last{half}", align_bytes=64) for half in range(2)]
-        wide_one = held.tile([P, 4 * C], BF16, name="wide_one", align_bytes=64)
-        wide_mid = held.tile([P, 4 * C], BF16, name="wide_mid", align_bytes=64)
+        g_all = [sbuf([P, PACK * S], F32, f"g_all{s}") for s in range(PASSES - 1)]
+        wide_pass0 = sbuf([P, PACK * S], BF16, "wide_pass0")
+        g_expert0 = sbuf([P, PACK * C], F32, "g_expert0")[:]
+        g_group3 = g_expert0[:, 0 : PACK * P]
+        g_group2 = sbuf([P, PACK * P], F32, "g_group2")
+        wide_expert0 = sbuf([P, PACK * C], BF16, "wide_expert0")
+        wide_group2 = sbuf([P, PACK * P], BF16, "wide_group2")
+        wide_group3 = sbuf([P, PACK * P], BF16, "wide_group3")
+        wide_pass1_e1 = sbuf([P, PACK * C], BF16, "wide_pass1_e1")
+        wide_pass1_e0 = sbuf([P, PACK * C], BF16, "wide_pass1_e0")
+        gate_group3 = gate_sb[:, C + P : S]
 
         for lo, hi in ((0, P), (P, S)):
             gather_row(0, 0, lo, hi - lo, gate_sb[:, lo:hi], g_all[0][:, lo:hi])
         gather(0, 0, S, gate_sb[:], g_all[0][:], (1, 2, 3))
-        interleave(wide_zero[:], g_all[0][:])
+        interleave(wide_pass0[:], g_all[0][:])
         gather(1, 0, S, gate_sb[:], g_all[1][:])
-        interleave(wide_mid[:], g_all[1][:], slice(0, C))
-        interleave(wide_one[:], g_all[1][:], slice(C, S))
-        quantize_g(0, 0, S, wide_zero[:], "dy1_1")
-        gather(2, 0, C, gate_first[:], g_first, (0, 1, 2))
-        quantize_g(1, 0, C, wide_mid[:], "gate_first")
-        gather(2, 0, C, gate_sb[:, 0:C], g_first, (3,))
-        interleave(wide_first[:], g_first)
-        gather(2, C, P, gate_late[:, 0:P], g_third[:])
-        interleave(wide_last[0][:], g_third[:])
-        gather(2, C + P, P, gate_late[:, P:C], g_last, (0,))
-        quantize_g(2, 0, C, wide_first[:])
-        gather(2, C + P, P, gate_late[:, P:C], g_last, (1, 2))
-        quantize_g(1, C, C, wide_one[:], "dy2_1")
-        gather(2, C + P, P, gate_late[:, P:C], g_last, (3,))
-        quantize_g(2, C, P, wide_last[0][:], "wide_one")
+        interleave(wide_pass1_e0[:], g_all[1][:], slice(0, C))
+        interleave(wide_pass1_e1[:], g_all[1][:], slice(C, S))
+        quantize_g(0, 0, S, wide_pass0[:], "dy1_1")
+        gather(2, 0, C, gate_first[:], g_expert0)
+        interleave(wide_expert0[:], g_expert0)
+        gather(2, C, P, gate_late[:], g_group2[:], (0,))
+        quantize_g(1, 0, C, wide_pass1_e0[:], "gate_first")
+        gather(2, C, P, gate_late[:], g_group2[:], (1, 2, 3))
+        interleave(wide_group2[:], g_group2[:])
+        quantize_g(2, 0, C, wide_expert0[:])
+        gather(2, C + P, P, gate_group3, g_group3, (0, 1))
+        quantize_g(1, C, C, wide_pass1_e1[:], "dy2_0")
+        gather(2, C + P, P, gate_group3, g_group3, (2, 3))
+        quantize_g(2, C, P, wide_group2[:], "wide_pass1_e1")
+
         multiply_w2(0, (0, 1))
         multiply_w2(0, (2, 3))
         multiply_w2(1, (0, 1))
         multiply_w2(2, (0, 1))
-        turn(0, 0)
+        turn(0, 0, wide_group3[:])
         turn(1, 0)
-        interleave(wide_last[1][:], g_last)
+        interleave(wide_group3[:], g_group3)
         multiply_w2(1, (2, 3))
         multiply_w2(2, (2,))
         make_mask(0, 0, "dy2_2")
         make_mask(1, 0, "dy2_3")
-        quantize_g(2, C + P, P, wide_last[1][:])
+        quantize_g(2, C + P, P, wide_group3[:])
         multiply_w2(2, (3,))
         turn(0, 1)
         turn(1, 1)
-        mask(0, 0, g_last.bitcast(BF16))
+
+        apply_mask(0, 0, g_group3.bitcast(BF16))
         make_mask(0, 1)
-        quantize_da(0, (0,), das[0, 0])
-        mask(0, 1, held.tile([P, 4 * C], BF16, name="da01", align_bytes=64)[:])
-        turn(2, 0)
-        turn(3, 0)
-        turn(2, 1)
-        turn(3, 1)
+        quantize_da(0, 0)
+        apply_mask(0, 1, sbuf([P, PACK * C], BF16, "da0_1")[:])
+        for h in range(HALVES):
+            turn(2, h)
+            turn(3, h)
         make_mask(1, 1)
-        quantize_da(0, (1,), das[0, 1])
-        mask(1, 0, held.tile([P, 4 * C], BF16, name="da10", tag="a_high0", align_bytes=64)[:])
-        mask(1, 1, held.tile([P, 4 * C], BF16, name="da11", align_bytes=64)[:])
-        quantize_da(1, (0,), das[1, 0], "dhb3_1")
-        quantize_da(1, (1,), das[1, 1])
-        for e in range(E):
-            multiply_w1(e)
+        quantize_da(0, 1)
+        apply_mask(1, 0, sbuf([P, PACK * C], BF16, "da1_0", "a_high1")[:])
+        apply_mask(1, 1, sbuf([P, PACK * C], BF16, "da1_1")[:])
+        quantize_da(1, 0, "rounded3_1")
+        quantize_da(1, 1)
+        for e, bank in enumerate(("bank3_1", "bank3_0")):
+            multiply_w1(e, bank)
             scatter(e)
         nc.sync.dma_start(out, window[:])

@@ -118,8 +118,8 @@ def tile_moe_bdx_mlp_relu_kernel(
                 g_codes[s, q] = codes[:, cols]
                 g_scales[s, q] = scales[:, cols]
 
-        def multiply_w2(s, groups):
-            for h in range(HALVES):
+        def multiply_w2(s, groups, halves=range(HALVES)):
+            for h in halves:
                 for q in groups:
                     e = q * P // C
                     if s == 0:
@@ -134,10 +134,10 @@ def tile_moe_bdx_mlp_relu_kernel(
                         stop=(s == PASSES - 1),
                     )
 
-        def turn(q, h, rounded=None):
+        def turn(q, h, rounded=None, bank=None):
             e = q * P // C
             if q % 2 == 0:
-                turned[e, h] = banks.tile([P, 2, C], F32, name="turned", tag=f"bank{q}_{h}")
+                turned[e, h] = banks.tile([P, 2, C], F32, name="turned", tag=bank or f"bank{q}_{h}")
             if rounded is None:
                 rounded = sbuf([P, SPAN], BF16, f"rounded{q}_{h}")[:]
             nc.scalar.copy(
@@ -188,15 +188,17 @@ def tile_moe_bdx_mlp_relu_kernel(
 
         g_all = [sbuf([P, PACK * S], F32, f"g_all{s}") for s in range(PASSES - 1)]
         wide_pass0 = sbuf([P, PACK * S], BF16, "wide_pass0")
-        g_expert0 = sbuf([P, PACK * C], F32, "g_expert0")[:]
-        g_group3 = g_expert0[:, 0 : PACK * P]
-        g_group2 = sbuf([P, PACK * P], F32, "g_group2")
-        wide_expert0 = sbuf([P, PACK * C], BF16, "wide_expert0")
-        wide_group2 = sbuf([P, PACK * P], BF16, "wide_group2")
-        wide_group3 = sbuf([P, PACK * P], BF16, "wide_group3")
-        wide_pass1_e1 = sbuf([P, PACK * C], BF16, "wide_pass1_e1")
         wide_pass1_e0 = sbuf([P, PACK * C], BF16, "wide_pass1_e0")
+        wide_pass1_e1 = sbuf([P, PACK * C], BF16, "wide_pass1_e1")
+        g_last = sbuf([P, 11 * P], F32, "g_last")
+        g_expert0 = g_last[:, 3 * P : 11 * P]
+        g_group2 = g_last[:, 0 : PACK * P]
+        g_group3 = g_last[:, 2 * P : 10 * P]
+        wide_group = [sbuf([P, PACK * P], BF16, f"wide_group{q}") for q in range(3)]
         gate_group3 = gate_sb[:, C + P : S]
+
+        def gather_group3(d):
+            gather_row(2, d, C + P, P, gate_group3, g_group3[:, d * C : d * C + P])
 
         for lo, hi in ((0, P), (P, S)):
             gather_row(0, 0, lo, hi - lo, gate_sb[:, lo:hi], g_all[0][:, lo:hi])
@@ -207,40 +209,47 @@ def tile_moe_bdx_mlp_relu_kernel(
         interleave(wide_pass1_e1[:], g_all[1][:], slice(C, S))
         quantize_g(0, 0, S, wide_pass0[:], "dy1_1")
         gather(2, 0, C, gate_first[:], g_expert0)
-        interleave(wide_expert0[:], g_expert0)
-        gather(2, C, P, gate_late[:], g_group2[:], (0,))
+        interleave(wide_group[0][:], g_expert0, slice(0, P))
+        interleave(wide_group[1][:], g_expert0, slice(P, C))
+        gather(2, C, P, gate_late[:], g_group2, (0,))
         quantize_g(1, 0, C, wide_pass1_e0[:], "gate_first")
-        gather(2, C, P, gate_late[:], g_group2[:], (1, 2, 3))
-        interleave(wide_group2[:], g_group2[:])
-        quantize_g(2, 0, C, wide_expert0[:])
-        gather(2, C + P, P, gate_group3, g_group3, (0, 1))
-        quantize_g(1, C, C, wide_pass1_e1[:], "dy2_0")
-        gather(2, C + P, P, gate_group3, g_group3, (2, 3))
-        quantize_g(2, C, P, wide_group2[:], "wide_pass1_e1")
+        gather(2, C, P, gate_late[:], g_group2, (1, 2))
+        quantize_g(2, 0, P, wide_group[0][:])
+        gather(2, C, P, gate_late[:], g_group2, (3,))
+        interleave(wide_group[2][:], g_group2)
+        quantize_g(2, P, P, wide_group[1][:])
+        gather_group3(3)
+        quantize_g(1, C, C, wide_pass1_e1[:], "wide_group1")
+        gather_group3(2)
+        gather_group3(1)
+        gather_group3(0)
+        quantize_g(2, C, P, wide_group[2][:])
 
         multiply_w2(0, (0, 1))
         multiply_w2(0, (2, 3))
         multiply_w2(1, (0, 1))
         multiply_w2(2, (0, 1))
-        turn(0, 0, wide_group3[:])
-        turn(1, 0)
-        interleave(wide_group3[:], g_group3)
         multiply_w2(1, (2, 3))
+        turn(0, 0)
+        turn(1, 0)
         multiply_w2(2, (2,))
-        make_mask(0, 0, "dy2_2")
-        make_mask(1, 0, "dy2_3")
+        turn(0, 1)
+        wide_group3 = sbuf([P, PACK * P], BF16, "wide_group3", "g_codes2_128")
+        interleave(wide_group3[:], g_group3, slice(0, P))
+        make_mask(0, 0, "dy2_0")
+        make_mask(1, 0, "wide_group2")
         quantize_g(2, C + P, P, wide_group3[:])
         multiply_w2(2, (3,))
-        turn(0, 1)
         turn(1, 1)
 
-        apply_mask(0, 0, g_group3.bitcast(BF16))
+        apply_mask(0, 0, g_group3[:, 0 : PACK * P].bitcast(BF16))
         make_mask(0, 1)
         quantize_da(0, 0)
         apply_mask(0, 1, sbuf([P, PACK * C], BF16, "da0_1")[:])
-        for h in range(HALVES):
-            turn(2, h)
-            turn(3, h)
+        turn(2, 0, None, "bank0_0")
+        turn(2, 1)
+        turn(3, 0)
+        turn(3, 1)
         make_mask(1, 1)
         quantize_da(0, 1)
         apply_mask(1, 0, sbuf([P, PACK * C], BF16, "da1_0", "a_high1")[:])

@@ -48,10 +48,10 @@ def tile_moe_bdx_mlp_relu_kernel(
         w1_planes = sbuf([P, E * HALVES, K], U8, "w1_planes")
         window = held.tile([P, T], F32, name="window")
         identity = held.tile([P, P], F32, name="identity")
-        nc.vector.memset(w2_planes[:].rearrange("p n c -> p (n c)").bitcast(I32), 0)
         nc.vector.memset(w1_planes[:].rearrange("p n c -> p (n c)").bitcast(I32), 0)
         nc.vector.memset(window[:], 0.0)
         make_identity(nc, identity[:])
+        nc.gpsimd.memset(w2_planes[:].rearrange("p n c -> p (n c)").bitcast(I32), 0)
 
         dy_view = dyT.rearrange("(s p d) t -> s d p t", p=P, d=PACK)
         dy = [[sbuf([P, T], F32, f"dy{s}_{d}") for d in range(PACK)] for s in range(PASSES)]
@@ -68,10 +68,10 @@ def tile_moe_bdx_mlp_relu_kernel(
             for d in rows:
                 nc.sync.dma_start(dy[s][d][:], dy_view[s, d])
 
-        def load_scales(planes, scales):
+        def load_scales(queue, planes, scales, rows=range(4)):
             by_row = scales.rearrange("e s (quad r) c -> r quad (e s) c", r=4)
-            for r in range(4):
-                nc.sync.dma_start(planes[r:P:32, :, :].bitcast(I32), by_row[r].bitcast(I32))
+            for r in rows:
+                queue.dma_start(planes[r:P:32, :, :].bitcast(I32), by_row[r].bitcast(I32))
 
         nc.sync.dma_start(offsets[:], offs)
         load_dy(0, (0,))
@@ -79,7 +79,8 @@ def tile_moe_bdx_mlp_relu_kernel(
         nc.sync.dma_start(gate_sb[:, P:S], gate[0:P, P:S])
         load_dy(0, (1, 2, 3))
         load_dy(1)
-        load_scales(w2_planes, w2_scales)
+        load_scales(nc.gpsimd, w2_planes, w2_scales, (0, 1, 2))
+        load_scales(nc.sync, w2_planes, w2_scales, (3,))
         load_dy(2, (0, 1))
         nc.sync.dma_start(w2_zero[:].bitcast(I32), w2_words[:, 0].rearrange("e p c -> p e c").bitcast(I32))
         load_dy(2, (2, 3))
@@ -90,7 +91,7 @@ def tile_moe_bdx_mlp_relu_kernel(
         for e in range(E):
             nc.sync.dma_start(a_high[e][:], a_view[1][:, :, e * C : (e + 1) * C])
         nc.sync.dma_start(w1_sb[:].bitcast(I32), w1_words.rearrange("e s p c -> p (e s) c").bitcast(I32))
-        load_scales(w1_planes, w1_scales)
+        load_scales(nc.sync, w1_planes, w1_scales)
         nc.scalar.copy(gate_first[:], gate_sb[:, 0:C])
 
         g_codes, g_scales, dh, turned, live, da, da_codes, da_scales, dx = {}, {}, {}, {}, {}, {}, {}, {}, {}

@@ -18,6 +18,7 @@ E4M3 = mybir.dt.float8_e4m3fn_x4
 E2M1 = mybir.dt.float4_e2m1fn_x4
 MULT = mybir.AluOpType.mult
 IS_GT = mybir.AluOpType.is_gt
+COPY = mybir.ActivationFunctionType.Copy
 
 P = 128
 PACK = 4
@@ -40,78 +41,98 @@ def tile_moe_bdx_mlp_relu_kernel(
             return held.tile(shape, dtype, name=name, tag=tag or name, align_bytes=MX_ALIGN)
 
         offsets = held.tile([P, S // LIST_ROWS], U16, name="offsets")
-
-        gate_sb = held.tile([P, S], F32, name="gate_sb")
-        gate_first = sbuf([P, C], F32, "gate_first")
-        gate_late = sbuf([P, P], F32, "gate_late")
-        w2_planes = sbuf([P, E * PASSES, H], U8, "w2_planes")
+        gate_sb = [sbuf([P, C], F32, f"gate_sb{e}") for e in range(E)]
+        w2_planes = [sbuf([P, PASSES, H], U8, f"w2_planes{e}") for e in range(E)]
         w1_planes = sbuf([P, E * HALVES, K], U8, "w1_planes")
         window = held.tile([P, T], F32, name="window")
         identity = held.tile([P, P], F32, name="identity")
+        for e in range(E):
+            nc.gpsimd.memset(w2_planes[e][:].rearrange("p n c -> p (n c)").bitcast(I32), 0)
         nc.vector.memset(w1_planes[:].rearrange("p n c -> p (n c)").bitcast(I32), 0)
         nc.vector.memset(window[:], 0.0)
         make_identity(nc, identity[:])
-        nc.gpsimd.memset(w2_planes[:].rearrange("p n c -> p (n c)").bitcast(I32), 0)
 
         dy_view = dyT.rearrange("(s p d) t -> s d p t", p=P, d=PACK)
         dy = [[sbuf([P, T], F32, f"dy{s}_{d}") for d in range(PACK)] for s in range(PASSES)]
-        w2_zero = sbuf([P, E, 2 * H], U8, "w2_zero")
-        w2_rest = [sbuf([P, PASSES - 1, 2 * H], U8, f"w2_rest{e}") for e in range(E)]
-        w2_sb = [[w2_zero[:, e, :], w2_rest[e][:, 0, :], w2_rest[e][:, 1, :]] for e in range(E)]
+        w2_sb = [[sbuf([P, 2 * H], U8, f"w2_{e}_{s}") for s in range(PASSES)] for e in range(E)]
         w1_sb = sbuf([P, E * HALVES, 2 * K], U8, "w1_sb")
-        a_low = sbuf([P, PACK, S], F32, "a_low")
-        a_high = [sbuf([P, PACK, C], F32, f"a_high{e}") for e in range(E)]
-        a_sb = [[a_low[:, :, e * C : (e + 1) * C], a_high[e][:]] for e in range(E)]
+        a_sb = {}
         a_view = a.rearrange("(h p d) c -> h p d c", p=P, d=PACK)
 
         def load_dy(s, rows=range(PACK)):
             for d in rows:
                 nc.sync.dma_start(dy[s][d][:], dy_view[s, d])
 
-        def load_scales(queue, planes, scales, rows=range(4)):
+        def load_w2(e, s):
+            nc.sync.dma_start(w2_sb[e][s][:].bitcast(I32), w2_words[e, s].bitcast(I32))
+
+        def load_a(h, lo, n):
+            rows = sbuf([P, PACK, n], F32, f"a{h}_{lo}")
+            nc.sync.dma_start(rows[:], a_view[h][:, :, lo : lo + n])
+            for q in range(lo // P, (lo + n) // P):
+                a_sb[q, h] = rows[:, :, q * P - lo : q * P - lo + P]
+
+        def load_scales(planes, scales, sets):
             by_row = scales.rearrange("e s (quad r) c -> r quad (e s) c", r=4)
-            for r in rows:
-                queue.dma_start(planes[r:P:32, :, :].bitcast(I32), by_row[r].bitcast(I32))
+            for r in range(4):
+                nc.sync.dma_start(planes[r:P:32, :, :].bitcast(I32), by_row[r][:, sets, :].bitcast(I32))
 
         nc.sync.dma_start(offsets[:], offs)
         load_dy(0, (0,))
-        nc.sync.dma_start(gate_sb[:, 0:P], gate[0:P, 0:P])
-        nc.sync.dma_start(gate_sb[:, P:S], gate[0:P, P:S])
+        nc.sync.dma_start(gate_sb[1][:], gate[0:P, C:S])
         load_dy(0, (1, 2, 3))
+        nc.sync.dma_start(gate_sb[0][:], gate[0:P, 0:C])
         load_dy(1)
-        load_scales(nc.gpsimd, w2_planes, w2_scales, (0, 1, 2))
-        load_scales(nc.sync, w2_planes, w2_scales, (3,))
+        load_scales(w2_planes[0], w2_scales, slice(0, PASSES))
+        load_w2(0, 0)
         load_dy(2, (0, 1))
-        nc.sync.dma_start(w2_zero[:].bitcast(I32), w2_words[:, 0].rearrange("e p c -> p e c").bitcast(I32))
+        load_w2(0, 1)
         load_dy(2, (2, 3))
-        nc.sync.dma_start(gate_late[:], gate[P : 2 * P, C : C + P])
-        for e in range(E):
-            nc.sync.dma_start(w2_rest[e][:].bitcast(I32), w2_words[e, 1:].rearrange("s p c -> p s c").bitcast(I32))
-        nc.sync.dma_start(a_low[:], a_view[0])
-        for e in range(E):
-            nc.sync.dma_start(a_high[e][:], a_view[1][:, :, e * C : (e + 1) * C])
+        load_scales(w2_planes[1], w2_scales, slice(PASSES, E * PASSES))
+        load_w2(1, 0)
+        load_w2(1, 1)
+        load_w2(0, 2)
+        load_w2(1, 2)
+        load_a(0, 0, C)
+        load_a(1, 0, C)
         nc.sync.dma_start(w1_sb[:].bitcast(I32), w1_words.rearrange("e s p c -> p (e s) c").bitcast(I32))
-        load_scales(nc.sync, w1_planes, w1_scales)
-        nc.scalar.copy(gate_first[:], gate_sb[:, 0:C])
+        load_scales(w1_planes, w1_scales, slice(0, E * HALVES))
+        load_a(0, C, C)
+        load_a(1, C, P)
+        load_a(1, C + P, P)
 
-        g_codes, g_scales, dh, turned, live, da, da_codes, da_scales, dx = {}, {}, {}, {}, {}, {}, {}, {}, {}
+        g_codes, g_scales, dh, turned, live, da, da_codes, da_scales = {}, {}, {}, {}, {}, {}, {}, {}
 
-        def gather_row(s, d, lo, n, gates, g_row):
-            picked = dy[s][d][:].indirect(offsets[:, lo // LIST_ROWS : (lo + n) // LIST_ROWS])
-            nc.vector.tensor_tensor(g_row, picked, gates, MULT)
+        rounded = {}
 
-        def gather(s, lo, n, gates, g, rows=range(PACK)):
-            for d in rows:
-                gather_row(s, d, lo, n, gates, g[:, d * n : (d + 1) * n])
+        def picked(s, d, lo, n):
+            return dy[s][d][:].indirect(offsets[:, lo // LIST_ROWS : (lo + n) // LIST_ROWS])
 
-        def interleave(wide, g, cols=slice(None)):
-            rows = g.rearrange("p (d c) -> p d c", d=PACK)[:, :, cols]
-            nc.scalar.copy(
-                wide.rearrange("p (c i d) -> p c d i", i=4, d=PACK), rows.rearrange("p d (c i) -> p c d i", i=4)
+        def gates(lo, n):
+            return gate_sb[lo // C][:, lo % C : lo % C + n]
+
+        def gather_gated(s, d, lo, n, rows):
+            nc.vector.tensor_tensor(rows[:, d * n : (d + 1) * n], picked(s, d, lo, n), gates(lo, n), MULT)
+
+        def gather_plain(s, d, lo, n, rows):
+            nc.scalar.activation(rows[:, d * n : (d + 1) * n], picked(s, d, lo, n), COPY)
+
+        def interleave(wide, rows):
+            nc.vector.tensor_copy(
+                wide.rearrange("p (c i d) -> p c d i", i=4, d=PACK), rows.rearrange("p (d c i) -> p c d i", d=PACK, i=4)
             )
 
-        def quantize_g(s, lo, n, wide, tag=None):
-            codes = sbuf([P, n], U32, f"g_codes{s}_{lo}", tag)
+        def gate_interleave(wide, rows, cols, lo, n):
+            by_row = rows.rearrange("p (d c) -> p d c", d=PACK)[:, :, cols]
+            nc.vector.tensor_tensor(
+                wide.rearrange("p (c i d) -> p c d i", i=2, d=PACK),
+                by_row.rearrange("p d (c i) -> p c d i", i=2),
+                gates(lo, n).rearrange("p (c i) -> p c i", i=2).unsqueeze(2).to_broadcast([P, n // 2, PACK, 2]),
+                MULT,
+            )
+
+        def quantize_g(s, lo, n, wide):
+            codes = sbuf([P, n], U32, f"g_codes{s}_{lo}")
             scales = sbuf([P, n], U8, f"g_scales{s}_{lo}")
             nc.vector.quantize_mx(out=codes[:].bitcast(E4M3), scales=scales[:], in_=wide)
             for q in range(lo // P, (lo + n) // P):
@@ -130,134 +151,152 @@ def tile_moe_bdx_mlp_relu_kernel(
                         lhsT=g_codes[s, q].bitcast(E4M3),
                         lhsT_scale=g_scales[s, q],
                         rhs=w2_sb[e][s][:, 2 * SPAN * h : 2 * SPAN * (h + 1)].bitcast(E2M1),
-                        rhs_scale=w2_planes[:, e * PASSES + s, SPAN * h : SPAN * (h + 1)],
+                        rhs_scale=w2_planes[e][:, s, SPAN * h : SPAN * (h + 1)],
                         start=(s == 0),
                         stop=(s == PASSES - 1),
                     )
 
-        def turn(q, h, rounded=None, bank=None):
-            e = q * P // C
-            if q % 2 == 0:
-                turned[e, h] = banks.tile([P, 2, C], F32, name="turned", tag=bank or f"bank{q}_{h}")
-            if rounded is None:
-                rounded = sbuf([P, SPAN], BF16, f"rounded{q}_{h}")[:]
+        def round_dh(q, h):
+            rounded[q, h] = sbuf([P, SPAN], BF16, f"rounded{q}_{h}")
             nc.scalar.copy(
-                rounded.rearrange("c (u p b) -> c u p b", u=2, b=2),
+                rounded[q, h][:].rearrange("c (u p b) -> c u p b", u=2, b=2),
                 dh[q, h][:].rearrange("c (p u b) -> c u p b", u=2, b=2),
             )
+
+        def turn(q, h, bank):
+            turned[q, h] = banks.tile([P, 2, P], F32, name="turned", tag=bank)
             for u in range(2):
-                words = rounded[:, 2 * P * u : 2 * P * (u + 1)].bitcast(F32)
-                nc.tensor.transpose(turned[e, h][:, u, q % 2 * P : (q % 2 + 1) * P], words, identity[:])
+                words = rounded[q, h][:, 2 * P * u : 2 * P * (u + 1)].bitcast(F32)
+                nc.tensor.transpose(turned[q, h][:, u, :], words, identity[:])
 
-        def make_mask(e, h, tag=None):
-            live[e, h] = sbuf([P, 2, C, 2], BF16, f"live{e}_{h}", tag)
-            nc.vector.tensor_scalar(live[e, h][:], a_sb[e][h].rearrange("p (u b) c -> p u c b", b=2), 0.0, None, IS_GT)
+        def make_mask(q, h):
+            live[q, h] = sbuf([P, 2, P, 2], BF16, f"live{q}_{h}")
+            nc.vector.tensor_scalar(live[q, h][:], a_sb[q, h].rearrange("p (u b) c -> p u c b", b=2), 0.0, None, IS_GT)
 
-        def apply_mask(e, h, product):
-            da[e, h] = product
+        def apply_mask(q, h, tag=None):
+            da[q, h] = sbuf([P, PACK * P], BF16, f"da{q}_{h}", tag)
             nc.vector.tensor_tensor(
-                product.rearrange("p (c u b) -> p c u b", u=2, b=2),
-                turned[e, h][:].rearrange("p u c -> p (u c)").bitcast(BF16).rearrange("p (u c b) -> p c u b", u=2, b=2),
-                live[e, h][:].rearrange("p u c b -> p c u b"),
+                da[q, h][:].rearrange("p (c u b) -> p c u b", u=2, b=2),
+                turned[q, h][:].rearrange("p u c -> p (u c)").bitcast(BF16).rearrange("p (u c b) -> p c u b", u=2, b=2),
+                live[q, h][:].rearrange("p u c b -> p c u b"),
                 MULT,
             )
 
-        def quantize_da(e, h, tag=None):
-            da_codes[e, h] = sbuf([P, C], U32, f"da_codes{e}_{h}", tag)
-            da_scales[e, h] = sbuf([P, C], U8, f"da_scales{e}_{h}")
-            nc.vector.quantize_mx(out=da_codes[e, h][:].bitcast(E4M3), scales=da_scales[e, h][:], in_=da[e, h])
+        def quantize_da(q, h):
+            if q % 2 == 0:
+                da_codes[q // 2, h] = sbuf([P, C], U32, f"da_codes{q}_{h}")
+                da_scales[q // 2, h] = sbuf([P, C], U8, f"da_scales{q}_{h}")
+            cols = slice(q % 2 * P, (q % 2 + 1) * P)
+            nc.vector.quantize_mx(
+                out=da_codes[q // 2, h][:, cols].bitcast(E4M3), scales=da_scales[q // 2, h][:, cols], in_=da[q, h][:]
+            )
 
-        def multiply_w1(e, bank):
-            dx[e] = banks.tile([P, C], F32, name="dx", tag=bank)
-            for cols in (slice(0, P), slice(P, C)):
-                for h in range(HALVES):
-                    nc.tensor.matmul_mx(
-                        out=dx[e][:, cols],
-                        lhsT=w1_sb[:, e * HALVES + h, :].bitcast(E2M1),
-                        lhsT_scale=w1_planes[:, e * HALVES + h, :],
-                        rhs=da_codes[e, h][:, cols].bitcast(E4M3),
-                        rhs_scale=da_scales[e, h][:, cols],
-                        start=(h == 0),
-                        stop=(h == HALVES - 1),
-                    )
+        def finish(lo, n, bank, copy):
+            e = lo // C
+            cols = slice(lo % C, lo % C + n)
+            dx = banks.tile([P, n], F32, name="dx", tag=bank)
+            for h in range(HALVES):
+                nc.tensor.matmul_mx(
+                    out=dx[:],
+                    lhsT=w1_sb[:, e * HALVES + h, :].bitcast(E2M1),
+                    lhsT_scale=w1_planes[:, e * HALVES + h, :],
+                    rhs=da_codes[e, h][:, cols].bitcast(E4M3),
+                    rhs_scale=da_scales[e, h][:, cols],
+                    start=(h == 0),
+                    stop=(h == HALVES - 1),
+                )
+            dx_sb = sbuf([P, n], F32, f"dx_sb{lo}")
+            copy(dx_sb[:], dx[:])
+            places = window[:].indirect(offsets[:, lo // LIST_ROWS : (lo + n) // LIST_ROWS])
+            nc.scalar.activation(places, dx_sb[:], COPY)
 
-        def scatter(e):
-            dx_sb = sbuf([P, C], F32, f"dx_sb{e}")
-            nc.scalar.copy(dx_sb[:], dx[e][:])
-            places = window[:].indirect(offsets[:, e * C // LIST_ROWS : (e + 1) * C // LIST_ROWS])
-            nc.vector.tensor_copy(places, dx_sb[:])
+        def rows_tile(name, n, tag=None):
+            return sbuf([P, PACK * n], F32, name, tag)[:]
 
-        g_all = [sbuf([P, PACK * S], F32, f"g_all{s}") for s in range(PASSES - 1)]
-        wide_pass0 = sbuf([P, PACK * S], BF16, "wide_pass0")
-        wide_pass1_e0 = sbuf([P, PACK * C], BF16, "wide_pass1_e0")
-        wide_pass1_e1 = sbuf([P, PACK * C], BF16, "wide_pass1_e1")
-        g_last = sbuf([P, 11 * P], F32, "g_last")
-        g_expert0 = g_last[:, 3 * P : 11 * P]
-        g_group2 = g_last[:, 0 : PACK * P]
-        g_group3 = g_last[:, 2 * P : 10 * P]
-        wide_group = [sbuf([P, PACK * P], BF16, f"wide_group{q}") for q in range(3)]
-        gate_group3 = gate_sb[:, C + P : S]
+        def wide_tile(name, n, tag=None):
+            return sbuf([P, PACK * n], BF16, name, tag)[:]
 
-        def gather_group3(d):
-            gather_row(2, d, C + P, P, gate_group3, g_group3[:, d * C : d * C + P])
-
-        for lo, hi in ((0, P), (P, S)):
-            gather_row(0, 0, lo, hi - lo, gate_sb[:, lo:hi], g_all[0][:, lo:hi])
-        gather(0, 0, S, gate_sb[:], g_all[0][:], (1, 2, 3))
-        interleave(wide_pass0[:], g_all[0][:])
-        gather(1, 0, S, gate_sb[:], g_all[1][:])
-        interleave(wide_pass1_e0[:], g_all[1][:], slice(0, C))
-        interleave(wide_pass1_e1[:], g_all[1][:], slice(C, S))
-        quantize_g(0, 0, S, wide_pass0[:], "dy1_1")
-        gather(2, 0, C, gate_first[:], g_expert0)
-        interleave(wide_group[0][:], g_expert0, slice(0, P))
-        interleave(wide_group[1][:], g_expert0, slice(P, C))
-        gather(2, C, P, gate_late[:], g_group2, (0,))
-        quantize_g(1, 0, C, wide_pass1_e0[:], "gate_first")
-        gather(2, C, P, gate_late[:], g_group2, (1, 2))
-        quantize_g(2, 0, P, wide_group[0][:])
-        gather(2, C, P, gate_late[:], g_group2, (3,))
-        interleave(wide_group[2][:], g_group2)
-        quantize_g(2, P, P, wide_group[1][:])
-        gather_group3(3)
-        quantize_g(1, C, C, wide_pass1_e1[:], "wide_group1")
-        gather_group3(2)
-        gather_group3(1)
-        gather_group3(0)
-        quantize_g(2, C, P, wide_group[2][:])
+        first, second = slice(0, PACK * P), slice(PACK * P, PACK * C)
+        rows_v0, rows_s0 = rows_tile("rows_v0", C), rows_tile("rows_s0", C)
+        for d in range(PACK):
+            gather_plain(0, d, 0, C, rows_s0)
+            gather_gated(0, d, C, C, rows_v0)
+        wide00, wide01 = wide_tile("wide00", C), wide_tile("wide01", C)
+        gate_interleave(wide00, rows_s0, slice(0, C), 0, C)
+        interleave(wide01, rows_v0)
+        quantize_g(0, 0, C, wide00)
+        rows_v1, rows_s1 = rows_tile("rows_v1", P), rows_tile("rows_s1", 3 * P)
+        rows_v2, rows_s2 = rows_tile("rows_v2", P), rows_tile("rows_s2", 3 * P)
+        gather_gated(1, 0, 0, P, rows_v1)
+        quantize_g(0, C, C, wide01)
+        for d in range(PACK):
+            gather_plain(1, d, P, 3 * P, rows_s1)
+        for d in range(1, PACK):
+            gather_gated(1, d, 0, P, rows_v1)
+        wide10 = wide_tile("wide10", C)
+        interleave(wide10[:, first], rows_v1)
+        gate_interleave(wide10[:, second], rows_s1, slice(0, P), P, P)
+        wide11 = wide_tile("wide11", C)
+        gate_interleave(wide11, rows_s1, slice(P, C + P), C, C)
+        quantize_g(1, 0, C, wide10)
+        gather_gated(2, 0, 0, P, rows_v2)
+        quantize_g(1, C, C, wide11)
+        for d in range(PACK):
+            gather_plain(2, d, P, 3 * P, rows_s2)
+        for d in range(1, PACK):
+            gather_gated(2, d, 0, P, rows_v2)
+        wide2_rest = wide_tile("wide2_rest", 3 * P, "rows_v2")
+        wide2 = [wide_tile("wide2_0", P)] + [wide2_rest[:, q * PACK * P : (q + 1) * PACK * P] for q in range(3)]
+        interleave(wide2[0], rows_v2)
+        quantize_g(2, 0, P, wide2[0])
+        gate_interleave(wide2[1], rows_s2, slice(0, P), P, P)
+        gate_interleave(wide2[2], rows_s2, slice(P, C), C, P)
+        quantize_g(2, P, P, wide2[1])
+        gate_interleave(wide2[3], rows_s2, slice(C, C + P), C + P, P)
+        quantize_g(2, C, P, wide2[2])
+        quantize_g(2, C + P, P, wide2[3])
 
         multiply_w2(0, (0, 1))
-        multiply_w2(0, (2, 3))
         multiply_w2(1, (0, 1))
-        multiply_w2(2, (0, 1))
+        multiply_w2(0, (2, 3))
         multiply_w2(1, (2, 3))
-        turn(0, 0)
-        turn(1, 0)
-        multiply_w2(2, (2,))
-        turn(0, 1)
-        wide_group3 = sbuf([P, PACK * P], BF16, "wide_group3", "g_codes2_128")
-        interleave(wide_group3[:], g_group3, slice(0, P))
-        make_mask(0, 0, "dy2_0")
-        make_mask(1, 0, "wide_group2")
-        quantize_g(2, C + P, P, wide_group3[:])
-        multiply_w2(2, (3,))
-        turn(1, 1)
-
-        apply_mask(0, 0, g_group3[:, 0 : PACK * P].bitcast(BF16))
-        make_mask(0, 1)
-        quantize_da(0, 0)
-        apply_mask(0, 1, sbuf([P, PACK * C], BF16, "da0_1")[:])
-        turn(2, 0, None, "bank0_0")
-        turn(2, 1)
-        turn(3, 0)
-        turn(3, 1)
-        make_mask(1, 1)
-        quantize_da(0, 1)
-        apply_mask(1, 0, sbuf([P, PACK * C], BF16, "da1_0", "a_high1")[:])
-        apply_mask(1, 1, sbuf([P, PACK * C], BF16, "da1_1")[:])
-        quantize_da(1, 0, "rounded3_1")
-        quantize_da(1, 1)
-        for e, bank in enumerate(("bank3_1", "bank3_0")):
-            multiply_w1(e, bank)
-            scatter(e)
+        for q in (0, 1):
+            multiply_w2(2, (q,))
+        for q in (0, 1):
+            for h in range(HALVES):
+                round_dh(q, h)
+            turn(q, 0, f"bank{q}_0")
+        for q in (2, 3):
+            multiply_w2(2, (q,))
+        for q in (2, 3):
+            for h in range(HALVES):
+                round_dh(q, h)
+        for step in (make_mask, apply_mask):
+            for q in (0, 1):
+                step(q, 0)
+        for q in (0, 1):
+            turn(q, 1, f"bank{q}_0")
+        for q in (2, 3):
+            for h in range(HALVES):
+                turn(q, h, f"bank{q}_{h}")
+        for q in (0, 1):
+            quantize_da(q, 0)
+        for step in (make_mask, apply_mask, quantize_da):
+            for q in (0, 1):
+                step(q, 1)
+        finish(0, C, "bank0_1", nc.scalar.copy)
+        make_mask(2, 0)
+        make_mask(3, 0)
+        apply_mask(2, 0)
+        quantize_da(2, 0)
+        make_mask(2, 1)
+        apply_mask(3, 0)
+        apply_mask(2, 1)
+        quantize_da(3, 0)
+        quantize_da(2, 1)
+        finish(C, P, "bank2_0", nc.scalar.copy)
+        make_mask(3, 1)
+        apply_mask(3, 1)
+        quantize_da(3, 1)
+        finish(C + P, P, "bank3_0", nc.vector.tensor_copy)
         nc.sync.dma_start(out, window[:])

@@ -42,12 +42,11 @@ def tile_moe_bdx_mlp_relu_kernel(
 
         offsets = held.tile([P, S // LIST_ROWS], U16, name="offsets")
         gate_sb = [sbuf([P, C], F32, f"gate_sb{e}") for e in range(E)]
-        w2_planes = [sbuf([P, PASSES, H], U8, f"w2_planes{e}") for e in range(E)]
+        w2_planes = sbuf([P, E * PASSES, H], U8, "w2_planes")
         w1_planes = sbuf([P, E * HALVES, K], U8, "w1_planes")
         window = held.tile([P, T], F32, name="window")
         identity = held.tile([P, P], F32, name="identity")
-        for e in range(E):
-            nc.gpsimd.memset(w2_planes[e][:].rearrange("p n c -> p (n c)").bitcast(I32), 0)
+        nc.gpsimd.memset(w2_planes[:].rearrange("p n c -> p (n c)").bitcast(I32), 0)
         nc.vector.memset(w1_planes[:].rearrange("p n c -> p (n c)").bitcast(I32), 0)
         nc.vector.memset(window[:], 0.0)
         make_identity(nc, identity[:])
@@ -72,23 +71,25 @@ def tile_moe_bdx_mlp_relu_kernel(
             for q in range(lo // P, (lo + n) // P):
                 a_sb[q, h] = rows[:, :, q * P - lo : q * P - lo + P]
 
-        def load_scales(planes, scales, sets):
+        def load_scales(queue, planes, scales, rows):
             by_row = scales.rearrange("e s (quad r) c -> r quad (e s) c", r=4)
-            for r in range(4):
-                nc.sync.dma_start(planes[r:P:32, :, :].bitcast(I32), by_row[r][:, sets, :].bitcast(I32))
+            for r in rows:
+                queue.dma_start(planes[r:P:32, :, :].bitcast(I32), by_row[r].bitcast(I32))
 
         nc.sync.dma_start(offsets[:], offs)
         load_dy(0, (0,))
         nc.sync.dma_start(gate_sb[1][:], gate[0:P, C:S])
         load_dy(0, (1, 2, 3))
         nc.sync.dma_start(gate_sb[0][:], gate[0:P, 0:C])
-        load_dy(1)
-        load_scales(w2_planes[0], w2_scales, slice(0, PASSES))
+        load_dy(1, (0, 1))
+        load_scales(nc.gpsimd, w2_planes, w2_scales, (0, 1))
+        load_scales(nc.gpsimd, w1_planes, w1_scales, range(4))
+        load_scales(nc.sync, w2_planes, w2_scales, (2, 3))
+        load_dy(1, (2, 3))
         load_w2(0, 0)
         load_dy(2, (0, 1))
         load_w2(0, 1)
         load_dy(2, (2, 3))
-        load_scales(w2_planes[1], w2_scales, slice(PASSES, E * PASSES))
         load_w2(1, 0)
         load_w2(1, 1)
         load_w2(0, 2)
@@ -96,7 +97,6 @@ def tile_moe_bdx_mlp_relu_kernel(
         load_a(0, 0, C)
         load_a(1, 0, C)
         nc.sync.dma_start(w1_sb[:].bitcast(I32), w1_words.rearrange("e s p c -> p (e s) c").bitcast(I32))
-        load_scales(w1_planes, w1_scales, slice(0, E * HALVES))
         load_a(0, C, C)
         load_a(1, C, P)
         load_a(1, C + P, P)
@@ -151,7 +151,7 @@ def tile_moe_bdx_mlp_relu_kernel(
                         lhsT=g_codes[s, q].bitcast(E4M3),
                         lhsT_scale=g_scales[s, q],
                         rhs=w2_sb[e][s][:, 2 * SPAN * h : 2 * SPAN * (h + 1)].bitcast(E2M1),
-                        rhs_scale=w2_planes[e][:, s, SPAN * h : SPAN * (h + 1)],
+                        rhs_scale=w2_planes[:, e * PASSES + s, SPAN * h : SPAN * (h + 1)],
                         start=(s == 0),
                         stop=(s == PASSES - 1),
                     )

@@ -54,7 +54,7 @@ def tile_moe_bdx_mlp_relu_kernel(
         dy_view = dyT.rearrange("(s p d) t -> s d p t", p=P, d=PACK)
         dy = [[sbuf([P, T], F32, f"dy{s}_{d}") for d in range(PACK)] for s in range(PASSES)]
         w2_sb = [[sbuf([P, 2 * H], U8, f"w2_{e}_{s}") for s in range(PASSES)] for e in range(E)]
-        w1_sb = sbuf([P, E * HALVES, 2 * K], U8, "w1_sb")
+        w1_sb = [sbuf([P, HALVES, 2 * K], U8, f"w1_{e}") for e in range(E)]
         a_sb = {}
         a_view = a.rearrange("(h p d) c -> h p d c", p=P, d=PACK)
 
@@ -64,6 +64,9 @@ def tile_moe_bdx_mlp_relu_kernel(
 
         def load_w2(e, s):
             nc.sync.dma_start(w2_sb[e][s][:].bitcast(I32), w2_words[e, s].bitcast(I32))
+
+        def load_w1(e):
+            nc.sync.dma_start(w1_sb[e][:].bitcast(I32), w1_words[e].rearrange("s p c -> p s c").bitcast(I32))
 
         def load_a(h, lo, n):
             rows = sbuf([P, PACK, n], F32, f"a{h}_{lo}")
@@ -76,8 +79,8 @@ def tile_moe_bdx_mlp_relu_kernel(
             for r in rows:
                 queue.dma_start(planes[r:P:32, :, :].bitcast(I32), by_row[r].bitcast(I32))
 
-        nc.sync.dma_start(offsets[:], offs)
         load_dy(0, (0,))
+        nc.sync.dma_start(offsets[:], offs)
         nc.sync.dma_start(gate_sb[1][:], gate[0:P, C:S])
         load_dy(0, (1, 2, 3))
         nc.sync.dma_start(gate_sb[0][:], gate[0:P, 0:C])
@@ -96,9 +99,10 @@ def tile_moe_bdx_mlp_relu_kernel(
         load_w2(1, 2)
         load_a(0, 0, C)
         load_a(1, 0, C)
-        nc.sync.dma_start(w1_sb[:].bitcast(I32), w1_words.rearrange("e s p c -> p (e s) c").bitcast(I32))
+        load_w1(0)
         load_a(0, C, C)
         load_a(1, C, P)
+        load_w1(1)
         load_a(1, C + P, P)
 
         g_codes, g_scales, dh, turned, live, da, da_codes, da_scales = {}, {}, {}, {}, {}, {}, {}, {}
@@ -156,9 +160,9 @@ def tile_moe_bdx_mlp_relu_kernel(
                         stop=(s == PASSES - 1),
                     )
 
-        def round_dh(q, h):
+        def round_dh(q, h, copy=nc.scalar.copy):
             rounded[q, h] = sbuf([P, SPAN], BF16, f"rounded{q}_{h}")
-            nc.scalar.copy(
+            copy(
                 rounded[q, h][:].rearrange("c (u p b) -> c u p b", u=2, b=2),
                 dh[q, h][:].rearrange("c (p u b) -> c u p b", u=2, b=2),
             )
@@ -198,7 +202,7 @@ def tile_moe_bdx_mlp_relu_kernel(
             for h in range(HALVES):
                 nc.tensor.matmul_mx(
                     out=dx[:],
-                    lhsT=w1_sb[:, e * HALVES + h, :].bitcast(E2M1),
+                    lhsT=w1_sb[e][:, h, :].bitcast(E2M1),
                     lhsT_scale=w1_planes[:, e * HALVES + h, :],
                     rhs=da_codes[e, h][:, cols].bitcast(E4M3),
                     rhs_scale=da_scales[e, h][:, cols],
@@ -263,8 +267,8 @@ def tile_moe_bdx_mlp_relu_kernel(
         for q in (0, 1):
             multiply_w2(2, (q,))
         for q in (0, 1):
-            for h in range(HALVES):
-                round_dh(q, h)
+            round_dh(q, 0, (nc.scalar.copy, nc.vector.tensor_copy)[q])
+            round_dh(q, 1)
             turn(q, 0, f"bank{q}_0")
         for q in (2, 3):
             multiply_w2(2, (q,))

@@ -96,8 +96,8 @@ def tile_moe_bdx_mlp_relu_kernel(
         load_w2(1, 0)
         load_w2(1, 1)
         load_w2(0, 2)
-        load_w2(1, 2)
         load_a(0, 0, C)
+        load_w2(1, 2)
         load_a(1, 0, C)
         load_w1(0)
         load_a(0, C, C)
@@ -264,12 +264,12 @@ def tile_moe_bdx_mlp_relu_kernel(
         multiply_w2(1, (0, 1))
         multiply_w2(0, (2, 3))
         multiply_w2(1, (2, 3))
+        multiply_w2(2, (0, 1))
         for q in (0, 1):
-            multiply_w2(2, (q,))
-        for q in (0, 1):
-            round_dh(q, 0, (nc.scalar.copy, nc.vector.tensor_copy)[q])
-            round_dh(q, 1)
+            round_dh(q, 0)
             turn(q, 0, f"bank{q}_0")
+        for q in (0, 1):
+            round_dh(q, 1)
         for q in (2, 3):
             multiply_w2(2, (q,))
         for q in (2, 3):

from contextlib import ExitStack

import concourse.mybir as mybir
from concourse.masks import make_identity

K, T, E, C, H, N = 128, 640, 2, 256, 1024, 1536
S = E * C
FLOPS = 2 * S * (N * H + H * K)
BYTES = 4 * (N * T + H * S + S + K * T) + E * (N * H + H * K) * 17 // 32 + 2 * S

F32 = mybir.dt.float32
BF16 = mybir.dt.bfloat16
U32 = mybir.dt.uint32
I32 = mybir.dt.int32
U16 = mybir.dt.uint16
U8 = mybir.dt.uint8
E4M3 = mybir.dt.float8_e4m3fn_x4
E2M1 = mybir.dt.float4_e2m1fn_x4
MULT = mybir.AluOpType.mult
IS_GT = mybir.AluOpType.is_gt
COPY = mybir.ActivationFunctionType.Copy

P = 128
PACK = 4
SPAN = P * PACK
PASSES = N // SPAN
HALVES = H // SPAN
LIST_ROWS = 16
MX_ALIGN = 64


def tile_moe_bdx_mlp_relu_kernel(
    tc, dyT, a, w2_words, w2_scales, w1_words, w1_scales, gate, offs, out
):
    nc = tc.nc
    with ExitStack() as ctx:
        held = ctx.enter_context(tc.tile_pool(name="held", bufs=1))
        banks = ctx.enter_context(tc.psum_pool(name="banks", bufs=1))

        def sbuf(shape, dtype, name, tag=None):
            return held.tile(shape, dtype, name=name, tag=tag or name, align_bytes=MX_ALIGN)

        offsets = held.tile([P, S // LIST_ROWS], U16, name="offsets")
        gate_sb = [sbuf([P, C], F32, f"gate_sb{e}") for e in range(E)]
        w2_planes = sbuf([P, E * PASSES, H], U8, "w2_planes")
        w1_planes = sbuf([P, E * HALVES, K], U8, "w1_planes")
        window = held.tile([P, T], F32, name="window")
        identity = held.tile([P, P], F32, name="identity")
        nc.gpsimd.memset(w2_planes[:].rearrange("p n c -> p (n c)").bitcast(I32), 0)
        nc.vector.memset(w1_planes[:].rearrange("p n c -> p (n c)").bitcast(I32), 0)
        nc.vector.memset(window[:], 0.0)
        make_identity(nc, identity[:])

        dy_view = dyT.rearrange("(s p d) t -> s d p t", p=P, d=PACK)
        dy = [[sbuf([P, T], F32, f"dy{s}_{d}") for d in range(PACK)] for s in range(PASSES)]
        w2_sb = [[sbuf([P, 2 * H], U8, f"w2_{e}_{s}") for s in range(PASSES)] for e in range(E)]
        w1_sb = [sbuf([P, HALVES, 2 * K], U8, f"w1_{e}") for e in range(E)]
        a_sb = {}
        a_view = a.rearrange("(h p d) c -> h p d c", p=P, d=PACK)

        def load_dy(s, rows=range(PACK)):
            for d in rows:
                nc.sync.dma_start(dy[s][d][:], dy_view[s, d])

        def load_w2(e, s):
            nc.sync.dma_start(w2_sb[e][s][:].bitcast(I32), w2_words[e, s].bitcast(I32))

        def load_w1(e):
            nc.sync.dma_start(w1_sb[e][:].bitcast(I32), w1_words[e].rearrange("s p c -> p s c").bitcast(I32))

        def load_a(h, lo, n):
            rows = sbuf([P, PACK, n], F32, f"a{h}_{lo}")
            nc.sync.dma_start(rows[:], a_view[h][:, :, lo : lo + n])
            for q in range(lo // P, (lo + n) // P):
                a_sb[q, h] = rows[:, :, q * P - lo : q * P - lo + P]

        def load_scales(queue, planes, scales, rows):
            by_row = scales.rearrange("e s (quad r) c -> r quad (e s) c", r=4)
            for r in rows:
                queue.dma_start(planes[r:P:32, :, :].bitcast(I32), by_row[r].bitcast(I32))

        load_dy(0, (0,))
        nc.sync.dma_start(offsets[:], offs)
        nc.sync.dma_start(gate_sb[1][:], gate[0:P, C:S])
        load_dy(0, (1, 2, 3))
        nc.sync.dma_start(gate_sb[0][:], gate[0:P, 0:C])
        load_dy(1, (0, 1))
        load_scales(nc.gpsimd, w2_planes, w2_scales, (0, 1))
        load_scales(nc.gpsimd, w1_planes, w1_scales, range(4))
        load_scales(nc.sync, w2_planes, w2_scales, (2, 3))
        load_dy(1, (2, 3))
        load_w2(0, 0)
        load_dy(2, (0, 1))
        load_w2(0, 1)
        load_dy(2, (2, 3))
        load_w2(1, 0)
        load_w2(1, 1)
        load_w2(0, 2)
        load_a(0, 0, C)
        load_w2(1, 2)
        load_a(1, 0, C)
        load_w1(0)
        load_a(0, C, C)
        load_a(1, C, P)
        load_w1(1)
        load_a(1, C + P, P)

        g_codes, g_scales, dh, turned, live, da, da_codes, da_scales = {}, {}, {}, {}, {}, {}, {}, {}

        rounded = {}

        def picked(s, d, lo, n):
            return dy[s][d][:].indirect(offsets[:, lo // LIST_ROWS : (lo + n) // LIST_ROWS])

        def gates(lo, n):
            return gate_sb[lo // C][:, lo % C : lo % C + n]

        def gather_gated(s, d, lo, n, rows):
            nc.vector.tensor_tensor(rows[:, d * n : (d + 1) * n], picked(s, d, lo, n), gates(lo, n), MULT)

        def gather_plain(s, d, lo, n, rows):
            nc.scalar.activation(rows[:, d * n : (d + 1) * n], picked(s, d, lo, n), COPY)

        def interleave(wide, rows):
            nc.vector.tensor_copy(
                wide.rearrange("p (c i d) -> p c d i", i=4, d=PACK), rows.rearrange("p (d c i) -> p c d i", d=PACK, i=4)
            )

        def gate_interleave(wide, rows, cols, lo, n):
            by_row = rows.rearrange("p (d c) -> p d c", d=PACK)[:, :, cols]
            nc.vector.tensor_tensor(
                wide.rearrange("p (c i d) -> p c d i", i=2, d=PACK),
                by_row.rearrange("p d (c i) -> p c d i", i=2),
                gates(lo, n).rearrange("p (c i) -> p c i", i=2).unsqueeze(2).to_broadcast([P, n // 2, PACK, 2]),
                MULT,
            )

        def quantize_g(s, lo, n, wide):
            codes = sbuf([P, n], U32, f"g_codes{s}_{lo}")
            scales = sbuf([P, n], U8, f"g_scales{s}_{lo}")
            nc.vector.quantize_mx(out=codes[:].bitcast(E4M3), scales=scales[:], in_=wide)
            for q in range(lo // P, (lo + n) // P):
                cols = slice(q * P - lo, q * P - lo + P)
                g_codes[s, q] = codes[:, cols]
                g_scales[s, q] = scales[:, cols]

        def multiply_w2(s, groups, halves=range(HALVES)):
            for h in halves:
                for q in groups:
                    e = q * P // C
                    if s == 0:
                        dh[q, h] = banks.tile([P, SPAN], F32, name="dh", tag=f"bank{q}_{h}")
                    nc.tensor.matmul_mx(
                        out=dh[q, h][:],
                        lhsT=g_codes[s, q].bitcast(E4M3),
                        lhsT_scale=g_scales[s, q],
                        rhs=w2_sb[e][s][:, 2 * SPAN * h : 2 * SPAN * (h + 1)].bitcast(E2M1),
                        rhs_scale=w2_planes[:, e * PASSES + s, SPAN * h : SPAN * (h + 1)],
                        start=(s == 0),
                        stop=(s == PASSES - 1),
                    )

        def round_dh(q, h, copy=nc.scalar.copy):
            rounded[q, h] = sbuf([P, SPAN], BF16, f"rounded{q}_{h}")
            copy(
                rounded[q, h][:].rearrange("c (u p b) -> c u p b", u=2, b=2),
                dh[q, h][:].rearrange("c (p u b) -> c u p b", u=2, b=2),
            )

        def turn(q, h, bank):
            turned[q, h] = banks.tile([P, 2, P], F32, name="turned", tag=bank)
            for u in range(2):
                words = rounded[q, h][:, 2 * P * u : 2 * P * (u + 1)].bitcast(F32)
                nc.tensor.transpose(turned[q, h][:, u, :], words, identity[:])

        def make_mask(q, h):
            live[q, h] = sbuf([P, 2, P, 2], BF16, f"live{q}_{h}")
            nc.vector.tensor_scalar(live[q, h][:], a_sb[q, h].rearrange("p (u b) c -> p u c b", b=2), 0.0, None, IS_GT)

        def apply_mask(q, h, tag=None):
            da[q, h] = sbuf([P, PACK * P], BF16, f"da{q}_{h}", tag)
            nc.vector.tensor_tensor(
                da[q, h][:].rearrange("p (c u b) -> p c u b", u=2, b=2),
                turned[q, h][:].rearrange("p u c -> p (u c)").bitcast(BF16).rearrange("p (u c b) -> p c u b", u=2, b=2),
                live[q, h][:].rearrange("p u c b -> p c u b"),
                MULT,
            )

        def quantize_da(q, h):
            if q % 2 == 0:
                da_codes[q // 2, h] = sbuf([P, C], U32, f"da_codes{q}_{h}")
                da_scales[q // 2, h] = sbuf([P, C], U8, f"da_scales{q}_{h}")
            cols = slice(q % 2 * P, (q % 2 + 1) * P)
            nc.vector.quantize_mx(
                out=da_codes[q // 2, h][:, cols].bitcast(E4M3), scales=da_scales[q // 2, h][:, cols], in_=da[q, h][:]
            )

        def finish(lo, n, bank, copy):
            e = lo // C
            cols = slice(lo % C, lo % C + n)
            dx = banks.tile([P, n], F32, name="dx", tag=bank)
            for h in range(HALVES):
                nc.tensor.matmul_mx(
                    out=dx[:],
                    lhsT=w1_sb[e][:, h, :].bitcast(E2M1),
                    lhsT_scale=w1_planes[:, e * HALVES + h, :],
                    rhs=da_codes[e, h][:, cols].bitcast(E4M3),
                    rhs_scale=da_scales[e, h][:, cols],
                    start=(h == 0),
                    stop=(h == HALVES - 1),
                )
            dx_sb = sbuf([P, n], F32, f"dx_sb{lo}")
            copy(dx_sb[:], dx[:])
            places = window[:].indirect(offsets[:, lo // LIST_ROWS : (lo + n) // LIST_ROWS])
            nc.scalar.activation(places, dx_sb[:], COPY)

        def rows_tile(name, n, tag=None):
            return sbuf([P, PACK * n], F32, name, tag)[:]

        def wide_tile(name, n, tag=None):
            return sbuf([P, PACK * n], BF16, name, tag)[:]

        first, second = slice(0, PACK * P), slice(PACK * P, PACK * C)
        rows_v0, rows_s0 = rows_tile("rows_v0", C), rows_tile("rows_s0", C)
        for d in range(PACK):
            gather_plain(0, d, 0, C, rows_s0)
            gather_gated(0, d, C, C, rows_v0)
        wide00, wide01 = wide_tile("wide00", C), wide_tile("wide01", C)
        gate_interleave(wide00, rows_s0, slice(0, C), 0, C)
        interleave(wide01, rows_v0)
        quantize_g(0, 0, C, wide00)
        rows_v1, rows_s1 = rows_tile("rows_v1", P), rows_tile("rows_s1", 3 * P)
        rows_v2, rows_s2 = rows_tile("rows_v2", P), rows_tile("rows_s2", 3 * P)
        gather_gated(1, 0, 0, P, rows_v1)
        quantize_g(0, C, C, wide01)
        for d in range(PACK):
            gather_plain(1, d, P, 3 * P, rows_s1)
        for d in range(1, PACK):
            gather_gated(1, d, 0, P, rows_v1)
        wide10 = wide_tile("wide10", C)
        interleave(wide10[:, first], rows_v1)
        gate_interleave(wide10[:, second], rows_s1, slice(0, P), P, P)
        wide11 = wide_tile("wide11", C)
        gate_interleave(wide11, rows_s1, slice(P, C + P), C, C)
        quantize_g(1, 0, C, wide10)
        gather_gated(2, 0, 0, P, rows_v2)
        quantize_g(1, C, C, wide11)
        for d in range(PACK):
            gather_plain(2, d, P, 3 * P, rows_s2)
        for d in range(1, PACK):
            gather_gated(2, d, 0, P, rows_v2)
        wide2_rest = wide_tile("wide2_rest", 3 * P, "rows_v2")
        wide2 = [wide_tile("wide2_0", P)] + [wide2_rest[:, q * PACK * P : (q + 1) * PACK * P] for q in range(3)]
        interleave(wide2[0], rows_v2)
        quantize_g(2, 0, P, wide2[0])
        gate_interleave(wide2[1], rows_s2, slice(0, P), P, P)
        gate_interleave(wide2[2], rows_s2, slice(P, C), C, P)
        quantize_g(2, P, P, wide2[1])
        gate_interleave(wide2[3], rows_s2, slice(C, C + P), C + P, P)
        quantize_g(2, C, P, wide2[2])
        quantize_g(2, C + P, P, wide2[3])

        multiply_w2(0, (0, 1))
        multiply_w2(1, (0, 1))
        multiply_w2(0, (2, 3))
        multiply_w2(1, (2, 3))
        multiply_w2(2, (0, 1))
        for q in (0, 1):
            round_dh(q, 0)
            turn(q, 0, f"bank{q}_0")
        for q in (0, 1):
            round_dh(q, 1)
        for q in (2, 3):
            multiply_w2(2, (q,))
        for q in (2, 3):
            for h in range(HALVES):
                round_dh(q, h)
        for step in (make_mask, apply_mask):
            for q in (0, 1):
                step(q, 0)
        for q in (0, 1):
            turn(q, 1, f"bank{q}_0")
        for q in (2, 3):
            for h in range(HALVES):
                turn(q, h, f"bank{q}_{h}")
        for q in (0, 1):
            quantize_da(q, 0)
        for step in (make_mask, apply_mask, quantize_da):
            for q in (0, 1):
                step(q, 1)
        finish(0, C, "bank0_1", nc.scalar.copy)
        make_mask(2, 0)
        make_mask(3, 0)
        apply_mask(2, 0)
        quantize_da(2, 0)
        make_mask(2, 1)
        apply_mask(3, 0)
        apply_mask(2, 1)
        quantize_da(3, 0)
        quantize_da(2, 1)
        finish(C, P, "bank2_0", nc.scalar.copy)
        make_mask(3, 1)
        apply_mask(3, 1)
        quantize_da(3, 1)
        finish(C + P, P, "bank3_0", nc.vector.tensor_copy)
        nc.sync.dma_start(out, window[:])
